import numpy as np
import ml_dtypes


def mxq(x, axis, fmt="e4m3"):
    dtype, down = {"e4m3": (ml_dtypes.float8_e4m3fn, 7), "e5m2": (ml_dtypes.float8_e5m2, 14)}[fmt]
    v = np.moveaxis(np.asarray(x, np.float32).astype(ml_dtypes.bfloat16).astype(np.float64), axis, -1)
    blocks = v.reshape(v.shape[:-1] + (-1, 32))
    amax = np.abs(blocks).max(-1, keepdims=True)
    byte = np.maximum(np.where(amax > 0, np.frexp(amax)[1] - 1 + 127, 0) - down, 1)
    scale = np.exp2(byte - 127.0)
    codes = (blocks / scale).astype(np.float32).astype(dtype).astype(np.float64)
    return np.moveaxis((codes * scale).reshape(v.shape), -1, axis)


WIDE = False


def mx_kscale(k):
    if not WIDE:
        return np.ones(k)
    levels = np.array([10, -10, 5, -5, 0])
    if k % 512:
        return np.exp2(np.random.permutation(np.resize(levels, k // 32))).repeat(32)
    a = np.empty((k // 512, 16))
    for p in range(k // 512):
        a[p, :8] = np.random.permutation(np.resize(levels, 8))
        for g in range(8):
            far = levels[np.abs(levels - a[p, g]) >= 10]
            a[p, g + 8] = far[np.random.randint(len(far))]
    return np.exp2(a.ravel()).repeat(32)


BF16 = ml_dtypes.bfloat16


def bf(x):
    return np.asarray(x, np.float32).astype(BF16)


def f64(x):
    return np.asarray(x).astype(np.float64)


E2M1 = np.array([0.0, 0.5, 1.0, 1.5, 2.0, 3.0, 4.0, 6.0, -0.0, -0.5, -1.0, -1.5, -2.0, -3.0, -4.0, -6.0])


def pack_weight(w, fmt):
    k, n = w.shape
    w = f64(bf(w)).reshape(k // 32, 32, n)
    amax = np.abs(w).max(1)
    if fmt == "e4m3":
        byte = np.frexp(amax)[1] - 1 + 127 - 7
    else:
        mant, ex = np.frexp(amax / 6.0)
        byte = np.where(mant > 0.5, ex, ex - 1) + 127
    byte = np.clip(np.where(amax > 0, byte, 1), 1, 254)
    scaled = (w * np.exp2(127.0 - byte)[:, None, :]).reshape(k, n).astype(np.float32)
    by_word = np.ascontiguousarray(scaled.reshape(k // 512, 128, 4, n).transpose(0, 1, 3, 2))
    if fmt == "e4m3":
        words = by_word.astype(ml_dtypes.float8_e4m3fn).view(np.uint8)
    else:
        c = by_word.astype(ml_dtypes.float4_e2m1fn).view(np.uint8) & 0xF
        words = c[..., 0::2] | (c[..., 1::2] << 4)
    return np.ascontiguousarray(words), np.ascontiguousarray(byte.astype(np.uint8).reshape(k // 512, 16, n))


def unpack_weight(words, scales, fmt):
    g, p, n, _ = words.shape
    if fmt == "e4m3":
        vals = np.ascontiguousarray(words).view(ml_dtypes.float8_e4m3fn).astype(np.float64)
    else:
        nib = np.empty((g, p, n, 4), np.uint8)
        nib[..., 0::2] = words & 0xF
        nib[..., 1::2] = words >> 4
        vals = E2M1[nib]
    vals = vals * np.repeat(np.exp2(scales.astype(np.float64) - 127.0), 8, axis=1)[..., None]
    return vals.transpose(0, 1, 3, 2).reshape(g * 512, n)
def pack4(w):
    words, scales = pack_weight(w, "e2m1")
    return words.reshape(words.shape[0], 128, -1), scales


def unpack4(words, scales):
    return unpack_weight(words.reshape(words.shape[0], 128, -1, 2), scales, "e2m1")


def planes(Y):
    n, m = Y.shape
    b = f64(bf(Y)).reshape(n // 32, 32, m)
    amax = np.abs(b).max(1)
    byte = np.clip(np.where(amax > 0, np.frexp(amax)[1] - 1 + 127 - 7, 1), 1, 254)
    codes = (b * np.exp2(127.0 - byte)[:, None, :]).reshape(n, m).astype(np.float32).astype(ml_dtypes.float8_e4m3fn).view(np.uint8)
    words = codes.reshape(n // 512, 128, 4, m).transpose(0, 1, 3, 2)
    return np.ascontiguousarray(words), np.ascontiguousarray(byte.astype(np.uint8).reshape(n // 512, 16, m))


B, HI, W, C, ND, P, O = 2, 4, 512, 1024, 512, 1024, 512


def softmax_last(t):
    e = np.exp(t - np.max(t, axis=-1, keepdims=True))
    return e / np.sum(e, axis=-1, keepdims=True)


def prime_context(x, wc_words, wc_scales, gw):
    y = mxq(f64(x), 3, "e4m3") @ unpack4(wc_words, wc_scales)
    m = np.max(y, axis=1)
    centred = m - np.mean(m, axis=-1, keepdims=True)
    return centred * f64(gw)[None, :, None]


def prime_depth(dl, gd):
    n_depth = dl.shape[-1]
    return (n_depth * softmax_last(f64(dl))) * f64(gd)[None, None, :]


def setup_inputs():
    s = mx_kscale(C)
    t = mx_kscale(ND)
    u = mx_kscale(W)
    x = bf(np.random.standard_normal((B, HI, W, C)) * s)
    wc_words, wc_scales = pack4(np.random.standard_normal((C, O)) / np.sqrt(C) / s[:, None])
    gw = bf((1.0 + 0.1 * np.random.standard_normal(W)) / u)
    dl = bf(1.5 * np.random.standard_normal((B, W, ND)))
    gd = bf(np.random.standard_normal(ND) * t)
    ring_words, ring_scales = pack4((np.random.standard_normal((P, ND)) / np.sqrt(ND) / t[None, :]).T)
    ray = bf(np.random.standard_normal((P, W)) / np.sqrt(W) * u[None, :])
    return {
        "x": x,
        "wc_words": wc_words,
        "wc_scales": wc_scales,
        "gw": gw,
        "dl": dl,
        "gd": gd,
        "ring_words": ring_words,
        "ring_scales": ring_scales,
        "ray": ray,
    }


def core(x, wc_words, wc_scales, gw, dl, gd, ring_words, ring_scales, ray):
    ctx = prime_context(x, wc_words, wc_scales, gw)
    d = prime_depth(dl, gd)
    rd = unpack4(ring_words, ring_scales).T @ mxq(d, 2, "e4m3").transpose(0, 2, 1)
    tm = rd * f64(ray)[None, :, :]
    return mxq(tm, 2, "e4m3") @ mxq(ctx, 1, "e4m3")


def reference(x, wc_words, wc_scales, gw, dl, gd, ring_words, ring_scales, ray):
    R_out = core(x, wc_words, wc_scales, gw, dl, gd, ring_words, ring_scales, ray)
    words, scales = planes(np.moveaxis(R_out, 2, 0).reshape(512, -1))
    return R_out, words, scales

@@ -1,0 +1,505 @@
+from contextlib import ExitStack
+
+import concourse.mybir as mybir
+from concourse.masks import make_identity
+
+F32 = mybir.dt.float32
+BF16 = mybir.dt.bfloat16
+I32 = mybir.dt.int32
+U32 = mybir.dt.uint32
+U8 = mybir.dt.uint8
+E4M3 = mybir.dt.float8_e4m3fn_x4
+E2M1 = mybir.dt.float4_e2m1fn_x4
+ALU = mybir.AluOpType
+ACT = mybir.ActivationFunctionType
+AX = mybir.AxisListType
+
+B, HI, W, C, ND, P, O = 2, 4, 512, 1024, 512, 1024, 512
+FLOPS = 2 * B * (HI * W * C * O + P * ND * W + P * W * O)
+STEPS = B * 4 * 2
+
+EXTRA = {0: [("ray", 0)], 1: [("ray", 1)], 3: [("d", 0)], 5: [("d", 1)]}
+XE = {}
+MAXS = {0: 0, 1: 1}
+EXPS = {1: (0, range(4)), 2: (1, (0, 1)), 3: (1, (2, 3))}
+NORM = {2: [(0, (0, 1))], 3: [(0, (2, 3))], 4: [(1, (0, 1))], 5: [(1, (2, 3))]}
+FILL = {
+    5: [("tm", 0, 0), ("tm", 0, 1)],
+    6: [("tm", 0, 2), ("tm", 0, 3), ("tm", 0, 4)],
+    7: [("tm", 0, 5), ("tm", 0, 6), ("tm", 0, 7)],
+    8: [("tm", 1, 0), ("tm", 1, 1)],
+    9: [("tm", 1, 2), ("tm", 1, 3), ("tm", 1, 4)],
+    10: [("tm", 1, 5), ("tm", 1, 6), ("tm", 1, 7), ("pl", 0, 0)],
+    11: [("pl", 0, 1), ("pl", 0, 2), ("pl", 0, 3)],
+    12: [("o", 0, 0), ("o", 0, 1), ("pl", 0, 4)],
+    13: [("pl", 0, 5), ("pl", 0, 6), ("pl", 0, 7)],
+    14: [("o", 0, 2), ("o", 0, 3)],
+    15: [("o", 0, 4)],
+}
+VEC_EVAC = {("pl", 0, 6)}
+
+
+def tile_matrixvtringraybev_x2_kernel(
+    tc, x, wc_words, wc_scales, gw, dl, gd, ring_words, ring_scales, ray, out_0, out_1, out_2
+):
+    nc = tc.nc
+    with ExitStack() as ctx:
+        keep = ctx.enter_context(tc.tile_pool(name="keep", bufs=1))
+        xin = ctx.enter_context(tc.tile_pool(name="xin", bufs=6))
+        two = ctx.enter_context(tc.tile_pool(name="two", bufs=2))
+        three = ctx.enter_context(tc.tile_pool(name="three", bufs=3))
+        ps_t = ctx.enter_context(tc.psum_pool(name="ps_t", bufs=2))
+        ps_y = ctx.enter_context(tc.psum_pool(name="ps_y", bufs=2))
+        ps_f = ctx.enter_context(tc.psum_pool(name="ps_f", bufs=4))
+        ctx.enter_context(tc.manual_schedule())
+
+        ident = keep.tile([128, 128], F32, name="ident")
+        make_identity(nc, ident[:])
+        wcw = keep.tile([128, 2 * 1024], U8, name="wcw", align_bytes=64)
+        wcs = keep.tile([128, 2, 512], U8, name="wcs", align_bytes=64)
+        ringw = keep.tile([128, 2048], U8, name="ringw", align_bytes=64)
+        rings = keep.tile([128, 1, 1024], U8, name="rings", align_bytes=64)
+        gz = keep.tile([128, 512], BF16, name="gz")
+        ones = keep.tile([128, 128], BF16, name="ones")
+        gd512 = keep.tile([128, 512], F32, name="gd512")
+        gwb = keep.tile([128, 4], BF16, name="gwb")
+        gw32 = keep.tile([128, 4], F32, name="gw32")
+        gwn = keep.tile([128, 4], F32, name="gwn")
+        rayin = keep.tile([128, 8 * 512], BF16, name="rayin")
+        rayg = keep.tile([128, 8 * 512], BF16, name="rayg")
+
+        nc.vector.memset(wcs[:].bitcast(U32), 0)
+        nc.vector.memset(gz[:], 0.0)
+        nc.vector.memset(ones[:], 1.0)
+        nc.vector.memset(rings[:].bitcast(U32), 0)
+
+        x_tiles = {}
+
+        def load_x(i, h0, hn):
+            b, t = divmod(i, 4)
+            if i not in x_tiles:
+                xt = xin.tile([128, 4 * 1024], BF16, name="xt")
+                x_tiles[i] = xt
+            nc.sync.dma_start(
+                out=x_tiles[i][:, 1024 * h0 : 1024 * (h0 + hn)].rearrange("m (h c) -> m h c", h=hn),
+                in_=x[b, h0 : h0 + hn, :, :].rearrange("h (m t) c -> t m h c", t=4)[t],
+            )
+
+        dlt = {}
+
+        def load_dl(b):
+            dl_t = two.tile([128, 4 * 512], BF16, name="dl_t")
+            dlt[b] = dl_t
+            nc.sync.dma_start(
+                out=dl_t[:].rearrange("m (t n) -> m t n", t=4),
+                in_=dl[b].rearrange("(m t) n -> m t n", t=4),
+            )
+
+        def load_scales(eng, plane, rows):
+            for q in range(4):
+                eng.dma_start(
+                    out=plane[32 * q : 32 * q + 4, :, :].bitcast(I32),
+                    in_=rows.bitcast(I32)[:, 4 * q : 4 * q + 4, :].rearrange("g q n -> q g n"),
+                )
+
+        def load_ray(j):
+            nc.sync.dma_start(
+                out=rayin[:, 2048 * j : 2048 * (j + 1)].rearrange("p (j w) -> p j w", j=4),
+                in_=ray[512 * j : 512 * (j + 1), :].rearrange("(j p) w -> p j w", p=128),
+            )
+
+        load_x(0, 0, 1)
+        load_x(0, 1, 1)
+        load_scales(nc.scalar, wcs, wc_scales)
+        nc.sync.dma_start(
+            out=wcw[:].bitcast(I32).rearrange("p (g n) -> p g n", g=2),
+            in_=wc_words.bitcast(I32).rearrange("g p n -> p g n"),
+        )
+        load_x(0, 2, 2)
+        nc.gpsimd.dma_start(out=gz[0:1, :], in_=gd.unsqueeze(0))
+        load_ray(0)
+        load_x(1, 0, 2)
+        load_dl(0)
+        nc.gpsimd.dma_start(out=gwb[:], in_=gw.rearrange("(m t) -> m t", t=4))
+        load_x(1, 2, 2)
+        load_ray(1)
+        load_x(2, 0, 4)
+        load_scales(nc.gpsimd, rings, ring_scales)
+        nc.sync.dma_start(out=ringw[:].bitcast(I32), in_=ring_words[0].bitcast(I32))
+        load_dl(1)
+        for i in range(3, 8):
+            load_x(i, 0, 4)
+
+        xp = {}
+        xg = {}
+        xq = {}
+
+        def x_transposes(s):
+            i, half = divmod(s, 2)
+            for hh in range(2):
+                bank = ps_t.tile([128, 512], F32, name="xp")
+                xp[s, hh] = bank
+                h = 2 * half + hh
+                words = x_tiles[i][:, 1024 * h : 1024 * (h + 1)].bitcast(F32)
+                for g in range(2):
+                    for u in range(2):
+                        k = 2 * g + u
+                        nc.tensor.transpose(
+                            bank[:, 128 * k : 128 * (k + 1)],
+                            words[:, 256 * g + u : 256 * (g + 1) : 2],
+                            ident[:],
+                        )
+
+        def copy_words(eng, out, bank, n):
+            src = bank.rearrange("p (a u r) -> p a r u", a=n, u=2)
+            dst = out.rearrange("p (a r u) -> p a r u", a=n, u=2)
+            if eng == "S":
+                nc.scalar.copy(out=dst, in_=src)
+            else:
+                nc.vector.tensor_copy(out=dst, in_=src)
+
+        def x_copies(s, engs="SS"):
+            g_t = three.tile([128, 2048], BF16, name="xg", align_bytes=64)
+            xg[s] = g_t
+            w = g_t[:].bitcast(F32)
+            for hh in range(2):
+                copy_words(engs[hh], w[:, 512 * hh : 512 * (hh + 1)], xp[s, hh][:], 2)
+
+        def quantize(pool, tag, src, cols):
+            codes = pool.tile([128, cols], U32, name=tag + "c", align_bytes=64)
+            scales = pool.tile([128, cols], U8, name=tag + "s", align_bytes=64)
+            nc.vector.quantize_mx(out=codes[:].bitcast(E4M3), scales=scales[:], in_=src)
+            return codes, scales
+
+        def x_quantize(s):
+            xq[s] = quantize(three, "xq", xg[s][:], 512)
+
+        ys = {}
+
+        def y_matmuls(s):
+            codes, scales = xq[s]
+            for hh in range(2):
+                bank = ps_y.tile([128, 512], F32, name="y")
+                ys[s, hh] = bank
+                for g in range(2):
+                    c = slice(256 * hh + 128 * g, 256 * hh + 128 * (g + 1))
+                    nc.tensor.matmul_mx(
+                        out=bank[:],
+                        lhsT=codes[:, c].bitcast(E4M3),
+                        lhsT_scale=scales[:, c],
+                        rhs=wcw[:, 1024 * g : 1024 * (g + 1)].bitcast(E2M1),
+                        rhs_scale=wcs[:, g, :],
+                        start=(g == 0),
+                        stop=(g == 1),
+                    )
+
+        ms = {}
+        msum = {}
+        ctxb = {}
+        cq = {}
+
+        def max_first(s):
+            i, half = divmod(s, 2)
+            if half == 0:
+                m_t = three.tile([128, 512], F32, name="m_t")
+                ms[i] = m_t
+                nc.scalar.copy(out=m_t[:], in_=ys[s, 0][:])
+            else:
+                nc.vector.tensor_tensor(out=ms[i][:], in0=ys[s, 0][:], in1=ms[i][:], op=ALU.max)
+
+        def max_second(s):
+            i, half = divmod(s, 2)
+            if half == 0:
+                nc.vector.tensor_tensor(out=ms[i][:], in0=ys[s, 1][:], in1=ms[i][:], op=ALU.max)
+            else:
+                sum_t = three.tile([128, 1], F32, name="sum_t")
+                msum[i] = sum_t
+                nc.vector.scalar_tensor_tensor(
+                    out=ms[i][:], in0=ys[s, 1][:], scalar=1.0, in1=ms[i][:],
+                    op0=ALU.mult, op1=ALU.max, accum_out=sum_t[:],
+                )
+
+        def centre(i):
+            b, t = divmod(i, 4)
+            if t == 0:
+                cb = two.tile([128, 4 * 512], BF16, name="cb")
+                ctxb[b] = cb
+            nb = three.tile([128, 1], F32, name="nb")
+            nc.scalar.activation(out=nb[:], in_=msum[i][:], func=ACT.Copy, scale=gwn[:, t : t + 1])
+            nc.scalar.activation(
+                out=ctxb[b][:, 512 * t : 512 * (t + 1)].rearrange("p (t m) -> p t m", t=4),
+                in_=ms[i][:].rearrange("p (m t) -> p t m", t=4),
+                func=ACT.Identity, scale=gw32[:, t : t + 1], bias=nb[:],
+            )
+
+        def ctx_interleave(b):
+            cg = two.tile([128, 4 * 512], BF16, name="cg", align_bytes=64)
+            ctxb[b, "g"] = cg
+            nc.vector.tensor_copy(
+                out=cg[:].rearrange("p (o t) -> p o t", t=4),
+                in_=ctxb[b][:].rearrange("p (t o) -> p o t", t=4),
+            )
+
+        def ctx_quantize(b):
+            cq[b] = quantize(two, "cq", ctxb[b, "g"][:], 512)
+
+        smx = {}
+
+        def sm_max(b):
+            d = dlt[b][:].rearrange("p (t n) -> p t n", t=4)
+            a1 = two.tile([128, 4, 256], BF16, name="a1", bufs=1)
+            a2 = two.tile([128, 4, 128], BF16, name="a2", bufs=1)
+            a3 = two.tile([128, 4, 64], BF16, name="a3", bufs=1)
+            mx = two.tile([128, 4], F32, name="mx")
+            nmx = two.tile([128, 4], F32, name="nmx")
+            nc.vector.tensor_tensor(out=a1[:], in0=d[:, :, 0:256], in1=d[:, :, 256:512], op=ALU.max)
+            nc.vector.tensor_tensor(out=a2[:], in0=a1[:, :, 0:128], in1=a1[:, :, 128:256], op=ALU.max)
+            nc.vector.tensor_tensor(out=a3[:], in0=a2[:, :, 0:64], in1=a2[:, :, 64:128], op=ALU.max)
+            nc.vector.tensor_reduce(out=mx[:], in_=a3[:], axis=AX.X, op=ALU.max)
+            nc.vector.tensor_scalar(out=nmx[:], in0=mx[:], scalar1=-1.0, scalar2=None, op0=ALU.mult)
+            e_t = two.tile([128, 4 * 512], F32, name="e_t")
+            es = two.tile([128, 4], F32, name="es")
+            smx[b] = (nmx, e_t, es)
+
+        def sm_exp(b, ts):
+            nmx, e_t, es = smx[b]
+            for t in ts:
+                nc.scalar.activation(
+                    out=e_t[:, 512 * t : 512 * (t + 1)].rearrange("p (u q e) -> p u q e", u=2, e=2),
+                    in_=dlt[b][:, 512 * t : 512 * (t + 1)].rearrange("p (q u e) -> p u q e", u=2, e=2),
+                    func=ACT.Exp, bias=nmx[:, t : t + 1], scale=1.0, accum_out=es[:, t : t + 1],
+                )
+
+        dg = {}
+        dxg = {}
+        dq = {}
+
+        def sm_norm(b, ts):
+            nmx, e_t, es = smx[b]
+            if 0 in ts:
+                ri = two.tile([128, 4], F32, name="ri")
+                nc.vector.reciprocal(out=ri[:], in_=es[:])
+                dgt = two.tile([128, 4 * 512], BF16, name="dgt", bufs=1)
+                dg[b] = dgt
+                smx[b, "ri"] = ri
+            for t in ts:
+                c = slice(512 * t, 512 * (t + 1))
+                nc.vector.scalar_tensor_tensor(
+                    out=dg[b][:, c], in0=e_t[:, c], scalar=smx[b, "ri"][:, t : t + 1], in1=gd512[:],
+                    op0=ALU.mult, op1=ALU.mult,
+                )
+
+        fb = {}
+
+        def extra_pe(unit):
+            kind, k = unit
+            for a in range(2):
+                bank = ps_f.tile([128, 512], F32, name="fb")
+                fb[unit, a] = bank
+                if kind == "ray":
+                    for jj in range(2):
+                        j = 4 * k + 2 * a + jj
+                        words = rayin[:, 512 * j : 512 * (j + 1)].bitcast(F32)
+                        for u in range(2):
+                            c = 2 * jj + u
+                            nc.tensor.transpose(bank[:, 128 * c : 128 * (c + 1)], words[:, u:256:2], ident[:])
+                else:
+                    words = dg[k][:].bitcast(F32)
+                    for c in range(4):
+                        src = 512 * a + 128 * c
+                        nc.tensor.transpose(
+                            bank[:, 128 * c : 128 * (c + 1)], words[:, src : src + 128], ident[:]
+                        )
+
+        def extra_evac(unit, engs):
+            kind, k = unit
+            if kind == "ray":
+                w = rayg[:].bitcast(F32)
+                for a in range(2):
+                    c = 1024 * k + 512 * a
+                    copy_words(engs[a], w[:, c : c + 512], fb[unit, a][:], 2)
+            else:
+                dx = two.tile([128, 4 * 512], BF16, name="dx", align_bytes=64, bufs=1)
+                dxg[k] = dx
+                w = dx[:].bitcast(F32)
+                for a in range(2):
+                    copy_words(engs[a], w[:, 512 * a : 512 * (a + 1)], fb[unit, a][:], 2)
+
+        tg = {}
+        tq = {}
+        pg = {}
+        pq = {}
+        ob = {}
+
+        def fill_pe(unit, where=0):
+            kind, b, j = unit
+            if where == 0:
+                bank = ps_f.tile([128, 512], F32, name="fb")
+            elif where == 1:
+                bank = ps_y.tile([128, 512], F32, name="y")
+            else:
+                bank = ps_t.tile([128, 512], F32, name="xp")
+            fb[unit] = bank
+            jc = slice(128 * j, 128 * (j + 1))
+            if kind == "o":
+                nc.tensor.matmul_mx(
+                    out=bank[:],
+                    lhsT=tq[b][0][:, jc].bitcast(E4M3), lhsT_scale=tq[b][1][:, jc],
+                    rhs=cq[b][0][:].bitcast(E4M3), rhs_scale=cq[b][1][:],
+                    start=True, stop=True,
+                )
+                return
+            for t in range(4):
+                c = slice(128 * t, 128 * (t + 1))
+                if kind == "tm":
+                    nc.tensor.matmul_mx(
+                        out=bank[:, c],
+                        lhsT=dq[b][0][:, c].bitcast(E4M3), lhsT_scale=dq[b][1][:, c],
+                        rhs=ringw[:, 256 * j : 256 * (j + 1)].bitcast(E2M1), rhs_scale=rings[:, 0, jc],
+                        start=True, stop=True,
+                    )
+                else:
+                    nc.tensor.matmul_mx(
+                        out=bank[:, c],
+                        lhsT=cq[b][0][:, c].bitcast(E4M3), lhsT_scale=cq[b][1][:, c],
+                        rhs=tq[b][0][:, jc].bitcast(E4M3), rhs_scale=tq[b][1][:, jc],
+                        start=True, stop=True,
+                    )
+
+        def fill_evac(unit, eng):
+            kind, b, j = unit
+            jj = j % 4
+            cols = slice(512 * jj, 512 * (jj + 1))
+            bank = fb[unit]
+            src = bank[:].rearrange("p (t n) -> p n t", t=4)
+            if kind == "tm":
+                if jj == 0:
+                    tgt = two.tile([128, 4 * 512], BF16, name="tgt", align_bytes=64)
+                    tg[b, j // 4] = tgt
+                nc.vector.tensor_tensor(
+                    out=tg[b, j // 4][:, cols].rearrange("p (n t) -> p n t", t=4),
+                    in0=src,
+                    in1=rayg[:, 512 * j : 512 * (j + 1)].rearrange("p (n t) -> p n t", t=4),
+                    op=ALU.mult,
+                )
+                return
+            if kind == "pl":
+                if jj == 0:
+                    pgt = two.tile([128, 4 * 512], BF16, name="pgt", align_bytes=64)
+                    pg[b, j // 4] = pgt
+                dst = pg[b, j // 4][:, cols]
+            else:
+                if jj == 0:
+                    obt = two.tile([128, 4 * 512], F32, name="obt")
+                    ob[b, j // 4] = obt
+                dst = ob[b, j // 4][:, cols]
+            dst = dst.rearrange("p (n t) -> p n t", t=4)
+            if eng == "S":
+                nc.scalar.copy(out=dst, in_=src)
+            else:
+                nc.vector.tensor_copy(out=dst, in_=src)
+            if kind == "o":
+                nc.sync.dma_start(out=out_0[b, 128 * j : 128 * (j + 1), :], in_=ob[b, j // 4][:, cols])
+
+        def fill_quantize(unit):
+            kind, b, j = unit
+            if kind == "o" or j % 4 != 3:
+                return
+            h = j // 4
+            c = slice(512 * h, 512 * (h + 1))
+            store, group, tag = (tq, tg, "tq") if kind == "tm" else (pq, pg, "pq")
+            if h == 0:
+                codes = two.tile([128, 1024], U32, name=tag + "c", align_bytes=64)
+                scales = two.tile([128, 1024], U8, name=tag + "s", align_bytes=64)
+                store[b] = (codes, scales)
+            codes, scales = store[b]
+            nc.vector.quantize_mx(out=codes[:, c].bitcast(E4M3), scales=scales[:, c], in_=group[b, h][:])
+            if kind == "pl":
+                m0 = 1024 * b + 512 * h
+                nc.sync.dma_start(
+                    out=out_1[0].rearrange("p m t -> p (m t)")[:, 4 * m0 : 4 * m0 + 2048].bitcast(I32),
+                    in_=codes[:, c].bitcast(I32),
+                )
+                if h == 1:
+                    for q in range(4):
+                        nc.sync.dma_start(
+                            out=out_2[0, 4 * q : 4 * q + 4, 1024 * b : 1024 * (b + 1)].bitcast(I32),
+                            in_=scales[32 * q : 32 * q + 4, :].bitcast(I32),
+                        )
+
+        x_transposes(0)
+        gdp = ps_f.tile([128, 512], F32, name="fb")
+        nc.tensor.matmul(gdp[:], ones[:], gz[:], start=True, stop=True)
+        x_copies(0, "SV")
+        x_quantize(0)
+        x_transposes(1)
+        nc.vector.tensor_copy(out=gw32[:], in_=gwb[:])
+        nc.vector.tensor_scalar(out=gwn[:], in0=gw32[:], scalar1=-1.0 / 512.0, scalar2=None, op0=ALU.mult)
+
+        last = []
+        last_x = []
+        for s in range(STEPS):
+            i, half = divmod(s, 2)
+            if s + 1 < STEPS:
+                x_copies(s + 1, "SV" if s == 0 else "SS")
+            y_matmuls(s)
+            for unit in last_x:
+                extra_evac(unit, XE.get(unit, "SS"))
+            for unit in last:
+                fill_evac(unit, "V" if unit in VEC_EVAC else "S")
+            if s == 0:
+                nc.scalar.activation(
+                    out=gd512[:].rearrange("p (u q e) -> p u q e", u=2, e=2),
+                    in_=gdp[:].rearrange("p (q u e) -> p u q e", u=2, e=2),
+                    func=ACT.Copy, scale=512.0,
+                )
+            if s in NORM:
+                for b_t in NORM[s]:
+                    sm_norm(*b_t)
+            if s == 9:
+                ctx_interleave(0)
+            max_first(s)
+            if half == 0 and s > 0:
+                centre(i - 1)
+            if s in EXPS:
+                sm_exp(*EXPS[s])
+            if s + 1 < STEPS:
+                x_quantize(s + 1)
+            max_second(s)
+            if s == 9:
+                ctx_quantize(0)
+            for unit in last_x:
+                if unit[0] == "d":
+                    dq[unit[1]] = quantize(two, "dq", dxg[unit[1]][:], 512)
+            for unit in last:
+                fill_quantize(unit)
+            if s in MAXS:
+                sm_max(MAXS[s])
+            for unit in FILL.get(s, []):
+                fill_pe(unit)
+            if s + 2 < STEPS:
+                x_transposes(s + 2)
+            for unit in EXTRA.get(s, []):
+                extra_pe(unit)
+            last = FILL.get(s, [])
+            last_x = EXTRA.get(s, [])
+
+        centre(7)
+        for unit in [("o", 0, 5), ("o", 0, 6), ("o", 0, 7)]:
+            fill_pe(unit)
+        for unit in last + [("o", 0, 5), ("o", 0, 6), ("o", 0, 7)]:
+            fill_evac(unit, "S")
+        ctx_interleave(1)
+        ctx_quantize(1)
+        order = []
+        for j in range(8):
+            order += [("pl", 1, j), ("o", 1, j)]
+        waiting = []
+        for n, unit in enumerate(order):
+            fill_pe(unit, (0, 1, 0, 2)[n % 4])
+            fill_evac(unit, "SVSSV"[n % 5])
+            for u in waiting:
+                fill_quantize(u)
+            waiting = [unit]
+        for u in waiting:
+            fill_quantize(u)

@@ -18,26 +18,7 @@ B, HI, W, C, ND, P, O = 2, 4, 512, 1024, 512, 1024, 512
 FLOPS = 2 * B * (HI * W * C * O + P * ND * W + P * W * O)
 STEPS = B * 4 * 2
 
-EXTRA = {0: [("ray", 0)], 1: [("ray", 1)], 3: [("d", 0)], 5: [("d", 1)]}
-XE = {}
-MAXS = {0: 0, 1: 1}
-EXPS = {1: (0, range(4)), 2: (1, (0, 1)), 3: (1, (2, 3))}
-NORM = {2: [(0, (0, 1))], 3: [(0, (2, 3))], 4: [(1, (0, 1))], 5: [(1, (2, 3))]}
-FILL = {
-    5: [("tm", 0, 0), ("tm", 0, 1)],
-    6: [("tm", 0, 2), ("tm", 0, 3), ("tm", 0, 4)],
-    7: [("tm", 0, 5), ("tm", 0, 6), ("tm", 0, 7)],
-    8: [("tm", 1, 0), ("tm", 1, 1)],
-    9: [("tm", 1, 2), ("tm", 1, 3), ("tm", 1, 4)],
-    10: [("tm", 1, 5), ("tm", 1, 6), ("tm", 1, 7), ("pl", 0, 0)],
-    11: [("pl", 0, 1), ("pl", 0, 2), ("pl", 0, 3)],
-    12: [("o", 0, 0), ("o", 0, 1), ("pl", 0, 4)],
-    13: [("pl", 0, 5), ("pl", 0, 6), ("pl", 0, 7)],
-    14: [("o", 0, 2), ("o", 0, 3)],
-    15: [("o", 0, 4)],
-}
-VEC_EVAC = {("pl", 0, 6)}
-
+PLAN = {'S': ['eXCyExbc', 'CyeExbcX'], 'V': ['eNEQBMMDMIMGMK', 'MNeIMEAKMQDBMGM'], 'fill': {4: [], 5: [('tm', 0, 0), ('tm', 0, 1), ('tm', 0, 2), ('tm', 0, 3)], 6: [('tm', 0, 4)], 7: [('tm', 0, 5)], 8: [], 9: [('tm', 0, 6), ('tm', 0, 7), ('tm', 1, 0), ('tm', 1, 1)], 10: [('tm', 1, 2), ('tm', 1, 3), ('tm', 1, 4)], 11: [('tm', 1, 5), ('pl', 0, 0), ('tm', 1, 6)], 12: [('tm', 1, 7), ('pl', 0, 1), ('pl', 0, 2), ('pl', 0, 3)], 13: [('o', 0, 0), ('o', 0, 1), ('o', 0, 2), ('pl', 0, 4)], 14: [('pl', 0, 5), ('pl', 0, 6), ('pl', 0, 7), ('o', 0, 3)], 15: [('o', 0, 4), ('o', 0, 5), ('o', 0, 6), ('o', 0, 7)]}, 'rest': [], 'extra': {3: [('d', 0)], 6: [('d', 1)], 0: [('ray', 0)], 1: [('ray', 1)]}, 'max': {0: 0, 2: 1}, 'exp': {3: (1, (0, 1)), 4: (1, (2, 3)), 2: (0, (0, 1, 2, 3))}, 'norm': {2: [(0, (0, 1))], 3: [(0, (2, 3))], 4: [(1, (0, 1))], 5: [(1, (2, 3))]}, 'vec': {('pl', 0, 2), ('o', 0, 1), ('pl', 0, 5), ('o', 0, 2)}, 'tail': 'VVSVSVSVSSSSSVVS', 'ctx': 9, 'xe': {('d', 1): 'SS', ('ray', 1): 'SS', ('ray', 0): 'SS', ('d', 0): 'SS'}}
 
 def tile_matrixvtringraybev_x2_kernel(
     tc, x, wc_words, wc_scales, gw, dl, gd, ring_words, ring_scales, ray, out_0, out_1, out_2
@@ -116,15 +97,15 @@ def tile_matrixvtringraybev_x2_kernel(
             in_=wc_words.bitcast(I32).rearrange("g p n -> p g n"),
         )
         load_x(0, 2, 2)
-        nc.gpsimd.dma_start(out=gz[0:1, :], in_=gd.unsqueeze(0))
+        nc.sync.dma_start(out=gz[0:1, :], in_=gd.unsqueeze(0))
         load_ray(0)
         load_x(1, 0, 2)
         load_dl(0)
-        nc.gpsimd.dma_start(out=gwb[:], in_=gw.rearrange("(m t) -> m t", t=4))
+        nc.sync.dma_start(out=gwb[:], in_=gw.rearrange("(m t) -> m t", t=4))
         load_x(1, 2, 2)
         load_ray(1)
         load_x(2, 0, 4)
-        load_scales(nc.gpsimd, rings, ring_scales)
+        load_scales(nc.sync, rings, ring_scales)
         nc.sync.dma_start(out=ringw[:].bitcast(I32), in_=ring_words[0].bitcast(I32))
         load_dl(1)
         for i in range(3, 8):
@@ -219,13 +200,19 @@ def tile_matrixvtringraybev_x2_kernel(
                     op0=ALU.mult, op1=ALU.max, accum_out=sum_t[:],
                 )
 
+        nbs = {}
+
+        def centre_bias(i):
+            nb = three.tile([128, 1], F32, name="nb")
+            nbs[i] = nb
+            nc.scalar.activation(out=nb[:], in_=msum[i][:], func=ACT.Copy, scale=gwn[:, i % 4 : i % 4 + 1])
+
         def centre(i):
             b, t = divmod(i, 4)
             if t == 0:
                 cb = two.tile([128, 4 * 512], BF16, name="cb")
                 ctxb[b] = cb
-            nb = three.tile([128, 1], F32, name="nb")
-            nc.scalar.activation(out=nb[:], in_=msum[i][:], func=ACT.Copy, scale=gwn[:, t : t + 1])
+            nb = nbs[i]
             nc.scalar.activation(
                 out=ctxb[b][:, 512 * t : 512 * (t + 1)].rearrange("p (t m) -> p t m", t=4),
                 in_=ms[i][:].rearrange("p (m t) -> p t m", t=4),
@@ -252,14 +239,18 @@ def tile_matrixvtringraybev_x2_kernel(
             a3 = two.tile([128, 4, 64], BF16, name="a3", bufs=1)
             mx = two.tile([128, 4], F32, name="mx")
             nmx = two.tile([128, 4], F32, name="nmx")
-            nc.vector.tensor_tensor(out=a1[:], in0=d[:, :, 0:256], in1=d[:, :, 256:512], op=ALU.max)
-            nc.vector.tensor_tensor(out=a2[:], in0=a1[:, :, 0:128], in1=a1[:, :, 128:256], op=ALU.max)
-            nc.vector.tensor_tensor(out=a3[:], in0=a2[:, :, 0:64], in1=a2[:, :, 64:128], op=ALU.max)
-            nc.vector.tensor_reduce(out=mx[:], in_=a3[:], axis=AX.X, op=ALU.max)
-            nc.vector.tensor_scalar(out=nmx[:], in0=mx[:], scalar1=-1.0, scalar2=None, op0=ALU.mult)
             e_t = two.tile([128, 4 * 512], F32, name="e_t")
             es = two.tile([128, 4], F32, name="es")
             smx[b] = (nmx, e_t, es)
+            return [
+                lambda: nc.vector.tensor_tensor(out=a1[:], in0=d[:, :, 0:256], in1=d[:, :, 256:512], op=ALU.max),
+                lambda: nc.vector.tensor_tensor(out=a2[:], in0=a1[:, :, 0:128], in1=a1[:, :, 128:256], op=ALU.max),
+                lambda: nc.vector.tensor_tensor(out=a3[:], in0=a2[:, :, 0:64], in1=a2[:, :, 64:128], op=ALU.max),
+                lambda: nc.vector.tensor_reduce(out=mx[:], in_=a3[:], axis=AX.X, op=ALU.max),
+                lambda: nc.vector.tensor_scalar(
+                    out=nmx[:], in0=mx[:], scalar1=-1.0, scalar2=None, op0=ALU.mult
+                ),
+            ]
 
         def sm_exp(b, ts):
             nmx, e_t, es = smx[b]
@@ -428,66 +419,102 @@ def tile_matrixvtringraybev_x2_kernel(
                         )
 
         x_transposes(0)
-        gdp = ps_f.tile([128, 512], F32, name="fb")
-        nc.tensor.matmul(gdp[:], ones[:], gz[:], start=True, stop=True)
         x_copies(0, "SV")
         x_quantize(0)
         x_transposes(1)
-        nc.vector.tensor_copy(out=gw32[:], in_=gwb[:])
-        nc.vector.tensor_scalar(out=gwn[:], in0=gw32[:], scalar1=-1.0 / 512.0, scalar2=None, op0=ALU.mult)
+        gdp = ps_f.tile([128, 512], F32, name="fb")
+        nc.tensor.matmul(gdp[:], ones[:], gz[:], start=True, stop=True)
 
         last = []
         last_x = []
         for s in range(STEPS):
             i, half = divmod(s, 2)
-            if s + 1 < STEPS:
-                x_copies(s + 1, "SV" if s == 0 else "SS")
+            v_evac = [u for u in last if u[0] == "tm" or u in PLAN["vec"]]
+            s_evac = [u for u in last if u not in v_evac]
             y_matmuls(s)
-            for unit in last_x:
-                extra_evac(unit, XE.get(unit, "SS"))
-            for unit in last:
-                fill_evac(unit, "V" if unit in VEC_EVAC else "S")
-            if s == 0:
-                nc.scalar.activation(
-                    out=gd512[:].rearrange("p (u q e) -> p u q e", u=2, e=2),
-                    in_=gdp[:].rearrange("p (q u e) -> p u q e", u=2, e=2),
-                    func=ACT.Copy, scale=512.0,
-                )
-            if s in NORM:
-                for b_t in NORM[s]:
-                    sm_norm(*b_t)
-            if s == 9:
-                ctx_interleave(0)
-            max_first(s)
-            if half == 0 and s > 0:
-                centre(i - 1)
-            if s in EXPS:
-                sm_exp(*EXPS[s])
-            if s + 1 < STEPS:
-                x_quantize(s + 1)
-            max_second(s)
-            if s == 9:
-                ctx_quantize(0)
-            for unit in last_x:
-                if unit[0] == "d":
-                    dq[unit[1]] = quantize(two, "dq", dxg[unit[1]][:], 512)
-            for unit in last:
-                fill_quantize(unit)
-            if s in MAXS:
-                sm_max(MAXS[s])
-            for unit in FILL.get(s, []):
+            for tok in PLAN["S"][half]:
+                if tok == "C" and s + 1 < STEPS:
+                    x_copies(s + 1, "SV" if s == 0 else "SS")
+                if tok == "x":
+                    for unit in last_x:
+                        extra_evac(unit, PLAN["xe"].get(unit, "SS"))
+                if tok == "y" and half == 0:
+                    max_first(s)
+                if tok == "y" and s == 0:
+                    nc.scalar.activation(
+                        out=gd512[:].rearrange("p (u q e) -> p u q e", u=2, e=2),
+                        in_=gdp[:].rearrange("p (q u e) -> p u q e", u=2, e=2),
+                        func=ACT.Copy, scale=512.0,
+                    )
+                if tok == "e":
+                    for unit in s_evac[:1]:
+                        fill_evac(unit, "S")
+                    s_evac = s_evac[1:]
+                if tok == "E":
+                    for unit in s_evac:
+                        fill_evac(unit, "S")
+                    s_evac = []
+                if tok == "b" and half == 0 and s > 0:
+                    centre_bias(i - 1)
+                if tok == "c" and half == 0 and s > 0:
+                    centre(i - 1)
+                if tok == "X" and s in PLAN["exp"]:
+                    sm_exp(*PLAN["exp"][s])
+            todo = []
+            if s in PLAN["max"]:
+                todo = sm_max(PLAN["max"][s])
+            if s == 1:
+                todo = [
+                    lambda: nc.vector.tensor_copy(out=gw32[:], in_=gwb[:]),
+                    lambda: nc.vector.tensor_scalar(out=gwn[:], in0=gw32[:], scalar1=-1.0 / 512.0, scalar2=None, op0=ALU.mult),
+                ]
+            for tok in PLAN["V"][half] + "MMMMM":
+                if tok == "Q" and s + 1 < STEPS:
+                    x_quantize(s + 1)
+                if tok == "A" and half == 1:
+                    max_first(s)
+                if tok == "B":
+                    max_second(s)
+                if tok == "e":
+                    for unit in v_evac[:1]:
+                        fill_evac(unit, "V")
+                    v_evac = v_evac[1:]
+                if tok == "E":
+                    for unit in v_evac:
+                        fill_evac(unit, "V")
+                    v_evac = []
+                if tok == "D":
+                    for unit in last_x:
+                        if unit[0] == "d":
+                            dq[unit[1]] = quantize(two, "dq", dxg[unit[1]][:], 512)
+                if tok == "I" and s == PLAN["ctx"]:
+                    ctx_interleave(0)
+                if tok == "G":
+                    for unit in last:
+                        fill_quantize(unit)
+                if tok == "K" and s == PLAN["ctx"]:
+                    ctx_quantize(0)
+                if tok == "M":
+                    if todo:
+                        todo.pop(0)()
+                if tok == "N":
+                    for b_t in PLAN["norm"].get(s, []):
+                        sm_norm(*b_t)
+            for unit in PLAN["fill"].get(s, []):
                 fill_pe(unit)
             if s + 2 < STEPS:
                 x_transposes(s + 2)
-            for unit in EXTRA.get(s, []):
+            for unit in PLAN["extra"].get(s, []):
                 extra_pe(unit)
-            last = FILL.get(s, [])
-            last_x = EXTRA.get(s, [])
+            last = PLAN["fill"].get(s, [])
+            last_x = PLAN["extra"].get(s, [])
 
+        rest = PLAN["rest"]
+        centre_bias(7)
         centre(7)
-        for unit in [("o", 0, 5), ("o", 0, 6), ("o", 0, 7)]:
-            fill_pe(unit)
-        for unit in last + [("o", 0, 5), ("o", 0, 6), ("o", 0, 7)]:
+        for n, unit in enumerate(rest):
+            fill_pe(unit, (1, 2)[n % 2])
+        for unit in last + rest:
             fill_evac(unit, "S")
         ctx_interleave(1)
         ctx_quantize(1)
@@ -497,7 +524,7 @@ def tile_matrixvtringraybev_x2_kernel(
         waiting = []
         for n, unit in enumerate(order):
             fill_pe(unit, (0, 1, 0, 2)[n % 4])
-            fill_evac(unit, "SVSSV"[n % 5])
+            fill_evac(unit, PLAN["tail"][n % len(PLAN["tail"])])
             for u in waiting:
                 fill_quantize(u)
             waiting = [unit]

@@ -14,519 +14,582 @@ ALU = mybir.AluOpType
 ACT = mybir.ActivationFunctionType
 AX = mybir.AxisListType
 
-B, HI, W, C, ND, P, O = 2, 4, 512, 1024, 512, 1024, 512
-FLOPS = 2 * B * (HI * W * C * O + P * ND * W + P * W * O)
-STEPS = B * 4 * 2
+BATCH, HEIGHTS, COLUMNS, FEATURES, BINS, CELLS, CHANNELS = 2, 4, 512, 1024, 512, 1024, 512
+FLOPS = 2 * BATCH * (HEIGHTS * COLUMNS * FEATURES * CHANNELS + CELLS * BINS * COLUMNS + CELLS * COLUMNS * CHANNELS)
 
-PLAN = {'S': ['eXCyExbc', 'CyeExbcX'], 'V': ['eNEQBMMDMIMGMK', 'MNeIMEAKMQDBMGM'], 'fill': {4: [], 5: [('tm', 0, 0), ('tm', 0, 1), ('tm', 0, 2), ('tm', 0, 3)], 6: [('tm', 0, 4)], 7: [('tm', 0, 5)], 8: [], 9: [('tm', 0, 6), ('tm', 0, 7), ('tm', 1, 0), ('tm', 1, 1)], 10: [('tm', 1, 2), ('tm', 1, 3), ('tm', 1, 4)], 11: [('tm', 1, 5), ('pl', 0, 0), ('tm', 1, 6)], 12: [('tm', 1, 7), ('pl', 0, 1), ('pl', 0, 2), ('pl', 0, 3)], 13: [('o', 0, 0), ('o', 0, 1), ('o', 0, 2), ('pl', 0, 4)], 14: [('pl', 0, 5), ('pl', 0, 6), ('pl', 0, 7), ('o', 0, 3)], 15: [('o', 0, 4), ('o', 0, 5), ('o', 0, 6), ('o', 0, 7)]}, 'rest': [], 'extra': {3: [('d', 0)], 6: [('d', 1)], 0: [('ray', 0)], 1: [('ray', 1)]}, 'max': {0: 0, 2: 1}, 'exp': {3: (1, (0, 1)), 4: (1, (2, 3)), 2: (0, (0, 1, 2, 3))}, 'norm': {2: [(0, (0, 1))], 3: [(0, (2, 3))], 4: [(1, (0, 1))], 5: [(1, (2, 3))]}, 'vec': {('pl', 0, 2), ('o', 0, 1), ('pl', 0, 5), ('o', 0, 2)}, 'tail': 'VVSVSVSVSSSSSVVS', 'ctx': 9, 'xe': {('d', 1): 'SS', ('ray', 1): 'SS', ('ray', 0): 'SS', ('d', 0): 'SS'}}
+PARTS = 128
+BANK = 512
+T = 4
+
+STEPS = BATCH * T * 2
+EARLY = 4
+
+TURNED = {0: ("ray", 0), 2: ("d", 0), 4: ("ray", 1), 6: ("d", 1)}
+EXPONENTIALS = {1: (0, 1), 3: (2, 3)}
+NORMALISED = {1: (0, (0, 1)), 2: (0, (2, 3)), 3: (1, (0, 1)), 6: (1, (2, 3))}
+CTX_STEP = 9
+UNITS = {
+    4: "tt", 5: "tt", 6: "t", 7: "t", 8: "t", 9: "tt", 10: "ptp", 11: "tptp",
+    12: "pto", 13: "oto", 14: "pppo", 15: "tot",
+}
+LEFT_OVER = "ooo"
+LAST_UNITS = "pooopooopopopppp"
+LAST_ENGINES = "VSSVSVSSVSVSSVSV"
+SORTED_STEPS = range(8, 15)
+
+SCALAR_EARLY = (
+    ("bias", "copy x", "height 0", "centre"),
+    ("copy x", "empty turned", "exponential"),
+)
+SCALAR_LATE = (
+    ("empty one", "sort x", "empty rest", "copy x", "bias", "height 0", "centre"),
+    ("empty one", "copy x", "empty rest", "empty turned", "sort x"),
+)
+VECTOR_EARLY = (
+    ("normalise", "small", "small", "small", "quantise x", "small", "second height", "small"),
+    ("small", "small", "first height", "quantise x", "second height", "quantise d", "normalise"),
+)
+VECTOR_LATE = (
+    ("empty one", "empty rest", "normalise", "quantise x", "second height", "quantise group"),
+    (
+        "empty one", "pack ctx", "empty rest", "first height", "quantise group", "quantise x",
+        "second height", "quantise ctx", "quantise d",
+    ),
+)
+
+
+def unit_list(letters, counts):
+    units = []
+    for letter in letters:
+        n = counts[letter]
+        counts[letter] = n + 1
+        units.append((letter, n // 8, n % 8))
+    return units
+
 
 def tile_matrixvtringraybev_x2_kernel(
     tc, x, wc_words, wc_scales, gw, dl, gd, ring_words, ring_scales, ray, out_0, out_1, out_2
 ):
     nc = tc.nc
-    with ExitStack() as ctx:
-        keep = ctx.enter_context(tc.tile_pool(name="keep", bufs=1))
-        xin = ctx.enter_context(tc.tile_pool(name="xin", bufs=6))
-        two = ctx.enter_context(tc.tile_pool(name="two", bufs=2))
-        three = ctx.enter_context(tc.tile_pool(name="three", bufs=3))
-        ps_t = ctx.enter_context(tc.psum_pool(name="ps_t", bufs=2))
-        ps_y = ctx.enter_context(tc.psum_pool(name="ps_y", bufs=2))
-        ps_f = ctx.enter_context(tc.psum_pool(name="ps_f", bufs=4))
-        ctx.enter_context(tc.manual_schedule())
+    with ExitStack() as stack:
+        pool = stack.enter_context(tc.tile_pool(name="sbuf", bufs=1))
+        psum = stack.enter_context(tc.psum_pool(name="psum", bufs=1))
+        stack.enter_context(tc.manual_schedule())
 
-        ident = keep.tile([128, 128], F32, name="ident")
+        made = {}
+
+        def rotating(name, count, shape, dtype, align=None):
+            n = made.get(name, 0)
+            made[name] = n + 1
+            if align is None:
+                tile = pool.tile(shape, dtype, name="%s%d" % (name, n % count))
+            else:
+                tile = pool.tile(shape, dtype, name="%s%d" % (name, n % count), align_bytes=align)
+            return tile
+
+        def bank_of(name, count):
+            n = made.get(name, 0)
+            made[name] = n + 1
+            bank = psum.tile([PARTS, BANK], F32, name="%s%d" % (name, n % count))
+            return bank
+
+        def turn_bank():
+            return bank_of("turn", 2)
+
+        def y_bank():
+            return bank_of("y", 2)
+
+        def unit_bank():
+            return bank_of("unit", 4)
+
+        ident = pool.tile([PARTS, PARTS], F32, name="ident")
         make_identity(nc, ident[:])
-        wcw = keep.tile([128, 2 * 1024], U8, name="wcw", align_bytes=64)
-        wcs = keep.tile([128, 2, 512], U8, name="wcs", align_bytes=64)
-        ringw = keep.tile([128, 2048], U8, name="ringw", align_bytes=64)
-        rings = keep.tile([128, 1, 1024], U8, name="rings", align_bytes=64)
-        gz = keep.tile([128, 512], BF16, name="gz")
-        ones = keep.tile([128, 128], BF16, name="ones")
-        gd512 = keep.tile([128, 512], F32, name="gd512")
-        gwb = keep.tile([128, 4], BF16, name="gwb")
-        gw32 = keep.tile([128, 4], F32, name="gw32")
-        gwn = keep.tile([128, 4], F32, name="gwn")
-        rayin = keep.tile([128, 8 * 512], BF16, name="rayin")
-        rayg = keep.tile([128, 8 * 512], BF16, name="rayg")
+        wc_codes = pool.tile([PARTS, 2 * 1024], U8, name="wc_codes", align_bytes=64)
+        wc_scale = pool.tile([PARTS, 2, 512], U8, name="wc_scale", align_bytes=64)
+        ring_codes = pool.tile([PARTS, 2048], U8, name="ring_codes", align_bytes=64)
+        ring_scale = pool.tile([PARTS, 1, 1024], U8, name="ring_scale", align_bytes=64)
+        gd_row = pool.tile([PARTS, BINS], BF16, name="gd_row")
+        ones = pool.tile([PARTS, PARTS], BF16, name="ones")
+        gd_512 = pool.tile([PARTS, BINS], F32, name="gd_512")
+        gw_bf16 = pool.tile([PARTS, T], BF16, name="gw_bf16")
+        gw_f32 = pool.tile([PARTS, T], F32, name="gw_f32")
+        gw_mean = pool.tile([PARTS, T], F32, name="gw_mean")
+        ray_in = pool.tile([PARTS, 8 * 512], BF16, name="ray_in")
+        ray_t = pool.tile([PARTS, 8 * 512], BF16, name="ray_t")
+        ctx_rows = pool.tile([PARTS, T * CHANNELS], BF16, name="ctx_rows")
 
-        nc.vector.memset(wcs[:].bitcast(U32), 0)
-        nc.vector.memset(gz[:], 0.0)
+        nc.vector.memset(wc_scale[:].bitcast(U32), 0)
+        nc.vector.memset(gd_row[:], 0.0)
         nc.vector.memset(ones[:], 1.0)
-        nc.vector.memset(rings[:].bitcast(U32), 0)
+        nc.vector.memset(ring_scale[:].bitcast(U32), 0)
 
-        x_tiles = {}
+        x_in = {}
+        dl_in = {}
 
-        def load_x(i, h0, hn):
-            b, t = divmod(i, 4)
-            if i not in x_tiles:
-                xt = xin.tile([128, 4 * 1024], BF16, name="xt")
-                x_tiles[i] = xt
+        def load_x(i, h0, count):
+            b, t = divmod(i, T)
+            if i not in x_in:
+                x_in[i] = rotating("x_in", 6, [PARTS, HEIGHTS * FEATURES], BF16)
             nc.sync.dma_start(
-                out=x_tiles[i][:, 1024 * h0 : 1024 * (h0 + hn)].rearrange("m (h c) -> m h c", h=hn),
-                in_=x[b, h0 : h0 + hn, :, :].rearrange("h (m t) c -> t m h c", t=4)[t],
+                out=x_in[i][:, FEATURES * h0 : FEATURES * (h0 + count)].rearrange("m (h c) -> m h c", h=count),
+                in_=x[b, h0 : h0 + count, :, :].rearrange("h (m t) c -> t m h c", t=T)[t],
             )
-
-        dlt = {}
 
         def load_dl(b):
-            dl_t = two.tile([128, 4 * 512], BF16, name="dl_t")
-            dlt[b] = dl_t
+            dl_in[b] = rotating("dl_in", 2, [PARTS, T * BINS], BF16)
             nc.sync.dma_start(
-                out=dl_t[:].rearrange("m (t n) -> m t n", t=4),
-                in_=dl[b].rearrange("(m t) n -> m t n", t=4),
+                out=dl_in[b][:].rearrange("m (t n) -> m t n", t=T),
+                in_=dl[b].rearrange("(m t) n -> m t n", t=T),
             )
 
-        def load_scales(eng, plane, rows):
+        def load_ray(half):
+            nc.sync.dma_start(
+                out=ray_in[:, 2048 * half : 2048 * (half + 1)].rearrange("p (j w) -> p j w", j=4),
+                in_=ray[512 * half : 512 * (half + 1), :].rearrange("(j p) w -> p j w", p=PARTS),
+            )
+
+        def load_scales(engine, scale, rows):
             for q in range(4):
-                eng.dma_start(
-                    out=plane[32 * q : 32 * q + 4, :, :].bitcast(I32),
+                engine.dma_start(
+                    out=scale[32 * q : 32 * q + 4, :, :].bitcast(I32),
                     in_=rows.bitcast(I32)[:, 4 * q : 4 * q + 4, :].rearrange("g q n -> q g n"),
                 )
 
-        def load_ray(j):
-            nc.sync.dma_start(
-                out=rayin[:, 2048 * j : 2048 * (j + 1)].rearrange("p (j w) -> p j w", j=4),
-                in_=ray[512 * j : 512 * (j + 1), :].rearrange("(j p) w -> p j w", p=128),
-            )
-
+        load_scales(nc.scalar, wc_scale, wc_scales)
         load_x(0, 0, 1)
+        load_dl(0)
         load_x(0, 1, 1)
-        load_scales(nc.scalar, wcs, wc_scales)
+        load_x(0, 2, 2)
+        nc.sync.dma_start(out=gd_row[0:1, :], in_=gd.unsqueeze(0))
         nc.sync.dma_start(
-            out=wcw[:].bitcast(I32).rearrange("p (g n) -> p g n", g=2),
+            out=wc_codes[:].bitcast(I32).rearrange("p (g n) -> p g n", g=2),
             in_=wc_words.bitcast(I32).rearrange("g p n -> p g n"),
         )
-        load_x(0, 2, 2)
-        nc.sync.dma_start(out=gz[0:1, :], in_=gd.unsqueeze(0))
-        load_ray(0)
         load_x(1, 0, 2)
-        load_dl(0)
-        nc.sync.dma_start(out=gwb[:], in_=gw.rearrange("(m t) -> m t", t=4))
-        load_x(1, 2, 2)
-        load_ray(1)
-        load_x(2, 0, 4)
-        load_scales(nc.sync, rings, ring_scales)
-        nc.sync.dma_start(out=ringw[:].bitcast(I32), in_=ring_words[0].bitcast(I32))
         load_dl(1)
+        load_x(1, 2, 2)
+        nc.sync.dma_start(out=gw_bf16[:], in_=gw.rearrange("(m t) -> m t", t=T))
+        load_ray(0)
+        nc.sync.dma_start(out=ring_codes[:].bitcast(I32), in_=ring_words[0].bitcast(I32))
+        load_scales(nc.sync, ring_scale, ring_scales)
+        load_x(2, 0, 4)
+        load_ray(1)
         for i in range(3, 8):
             load_x(i, 0, 4)
 
-        xp = {}
-        xg = {}
-        xq = {}
+        def quantise(tag, count, rows, columns):
+            codes = rotating(tag + "_codes", count, [PARTS, columns], U32, 64)
+            scale = rotating(tag + "_scale", count, [PARTS, columns], U8, 64)
+            nc.vector.quantize_mx(out=codes[:].bitcast(E4M3), scales=scale[:], in_=rows)
+            return codes, scale
 
-        def x_transposes(s):
-            i, half = divmod(s, 2)
-            for hh in range(2):
-                bank = ps_t.tile([128, 512], F32, name="xp")
-                xp[s, hh] = bank
-                h = 2 * half + hh
-                words = x_tiles[i][:, 1024 * h : 1024 * (h + 1)].bitcast(F32)
-                for g in range(2):
-                    for u in range(2):
-                        k = 2 * g + u
-                        nc.tensor.transpose(
-                            bank[:, 128 * k : 128 * (k + 1)],
-                            words[:, 256 * g + u : 256 * (g + 1) : 2],
-                            ident[:],
-                        )
-
-        def copy_words(eng, out, bank, n):
-            src = bank.rearrange("p (a u r) -> p a r u", a=n, u=2)
-            dst = out.rearrange("p (a r u) -> p a r u", a=n, u=2)
-            if eng == "S":
-                nc.scalar.copy(out=dst, in_=src)
+        def copy_words(engine, out, bank):
+            source = bank.rearrange("p (a u r) -> p a r u", a=2, u=2)
+            target = out.rearrange("p (a r u) -> p a r u", a=2, u=2)
+            if engine == "S":
+                nc.scalar.copy(out=target, in_=source)
             else:
-                nc.vector.tensor_copy(out=dst, in_=src)
+                nc.vector.tensor_copy(out=target, in_=source)
 
-        def x_copies(s, engs="SS"):
-            g_t = three.tile([128, 2048], BF16, name="xg", align_bytes=64)
-            xg[s] = g_t
-            w = g_t[:].bitcast(F32)
-            for hh in range(2):
-                copy_words(engs[hh], w[:, 512 * hh : 512 * (hh + 1)], xp[s, hh][:], 2)
+        x_sorted = {}
+        x_banks = {}
+        x_packed = {}
+        x_quant = {}
+        y_banks = {}
 
-        def quantize(pool, tag, src, cols):
-            codes = pool.tile([128, cols], U32, name=tag + "c", align_bytes=64)
-            scales = pool.tile([128, cols], U8, name=tag + "s", align_bytes=64)
-            nc.vector.quantize_mx(out=codes[:].bitcast(E4M3), scales=scales[:], in_=src)
-            return codes, scales
-
-        def x_quantize(s):
-            xq[s] = quantize(three, "xq", xg[s][:], 512)
-
-        ys = {}
-
-        def y_matmuls(s):
-            codes, scales = xq[s]
-            for hh in range(2):
-                bank = ps_y.tile([128, 512], F32, name="y")
-                ys[s, hh] = bank
-                for g in range(2):
-                    c = slice(256 * hh + 128 * g, 256 * hh + 128 * (g + 1))
-                    nc.tensor.matmul_mx(
-                        out=bank[:],
-                        lhsT=codes[:, c].bitcast(E4M3),
-                        lhsT_scale=scales[:, c],
-                        rhs=wcw[:, 1024 * g : 1024 * (g + 1)].bitcast(E2M1),
-                        rhs_scale=wcs[:, g, :],
-                        start=(g == 0),
-                        stop=(g == 1),
-                    )
-
-        ms = {}
-        msum = {}
-        ctxb = {}
-        cq = {}
-
-        def max_first(s):
+        def x_words(s, hh):
             i, half = divmod(s, 2)
-            if half == 0:
-                m_t = three.tile([128, 512], F32, name="m_t")
-                ms[i] = m_t
-                nc.scalar.copy(out=m_t[:], in_=ys[s, 0][:])
-            else:
-                nc.vector.tensor_tensor(out=ms[i][:], in0=ys[s, 0][:], in1=ms[i][:], op=ALU.max)
+            h = 2 * half + hh
+            return x_in[i][:, FEATURES * h : FEATURES * (h + 1)].bitcast(F32)
 
-        def max_second(s):
-            i, half = divmod(s, 2)
-            if half == 0:
-                nc.vector.tensor_tensor(out=ms[i][:], in0=ys[s, 1][:], in1=ms[i][:], op=ALU.max)
-            else:
-                sum_t = three.tile([128, 1], F32, name="sum_t")
-                msum[i] = sum_t
-                nc.vector.scalar_tensor_tensor(
-                    out=ms[i][:], in0=ys[s, 1][:], scalar=1.0, in1=ms[i][:],
-                    op0=ALU.mult, op1=ALU.max, accum_out=sum_t[:],
+        def sort_x(s):
+            if s in SORTED_STEPS:
+                x_sorted[s] = rotating("x_sorted", 3, [PARTS, FEATURES], BF16)
+                nc.scalar.copy(
+                    out=x_sorted[s][:].bitcast(F32).rearrange("p (g u r) -> p g u r", g=2, u=2),
+                    in_=x_words(s, 1).rearrange("p (g r u) -> p g u r", g=2, u=2),
                 )
 
-        nbs = {}
+        def turn_x(s):
+            for hh in range(2):
+                bank = turn_bank()
+                x_banks[s, hh] = bank
+                for n in range(4):
+                    g, u = divmod(n, 2)
+                    if hh == 1 and s in x_sorted:
+                        source = x_sorted[s][:].bitcast(F32)[:, PARTS * n : PARTS * (n + 1)]
+                    else:
+                        source = x_words(s, hh)[:, 256 * g + u : 256 * (g + 1) : 2]
+                    nc.tensor.transpose(bank[:, PARTS * n : PARTS * (n + 1)], source, ident[:])
+
+        def copy_x(s, engine):
+            x_packed[s] = rotating("x_packed", 4, [PARTS, 2 * FEATURES], BF16, 64)
+            words = x_packed[s][:].bitcast(F32)
+            for hh in range(2):
+                copy_words(engine, words[:, BANK * hh : BANK * (hh + 1)], x_banks[s, hh][:])
+
+        def quantise_x(s):
+            x_quant[s] = quantise("x", 3, x_packed[s][:], 512)
+
+        def multiply_y(s):
+            codes, scale = x_quant[s]
+            for hh in range(2):
+                bank = y_bank()
+                y_banks[s, hh] = bank
+                for g in range(2):
+                    c = slice(256 * hh + PARTS * g, 256 * hh + PARTS * (g + 1))
+                    nc.tensor.matmul_mx(
+                        out=bank[:],
+                        lhsT=codes[:, c].bitcast(E4M3), lhsT_scale=scale[:, c],
+                        rhs=wc_codes[:, 1024 * g : 1024 * (g + 1)].bitcast(E2M1), rhs_scale=wc_scale[:, g, :],
+                        start=(g == 0), stop=(g == 1),
+                    )
+
+        maximum = {}
+        channel_sum = {}
+        bias = {}
+        ctx_packed = {}
+        ctx_quant = {}
+
+        def height_zero(i):
+            maximum[i] = rotating("maximum", 3, [PARTS, CHANNELS], F32)
+            nc.scalar.copy(out=maximum[i][:], in_=y_banks[2 * i, 0][:])
+
+        def next_height(i, s, hh):
+            nc.vector.tensor_tensor(out=maximum[i][:], in0=y_banks[s, hh][:], in1=maximum[i][:], op=ALU.max)
+
+        def last_height(i, s):
+            channel_sum[i] = rotating("channel_sum", 3, [PARTS, 1], F32)
+            nc.vector.scalar_tensor_tensor(
+                out=maximum[i][:], in0=y_banks[s, 1][:], scalar=1.0, in1=maximum[i][:],
+                op0=ALU.mult, op1=ALU.max, accum_out=channel_sum[i][:],
+            )
 
         def centre_bias(i):
-            nb = three.tile([128, 1], F32, name="nb")
-            nbs[i] = nb
-            nc.scalar.activation(out=nb[:], in_=msum[i][:], func=ACT.Copy, scale=gwn[:, i % 4 : i % 4 + 1])
+            t = i % T
+            bias[i] = rotating("bias", 3, [PARTS, 1], F32)
+            nc.scalar.activation(
+                out=bias[i][:], in_=channel_sum[i][:], func=ACT.Copy, scale=gw_mean[:, t : t + 1]
+            )
 
         def centre(i):
-            b, t = divmod(i, 4)
-            if t == 0:
-                cb = two.tile([128, 4 * 512], BF16, name="cb")
-                ctxb[b] = cb
-            nb = nbs[i]
+            t = i % T
             nc.scalar.activation(
-                out=ctxb[b][:, 512 * t : 512 * (t + 1)].rearrange("p (t m) -> p t m", t=4),
-                in_=ms[i][:].rearrange("p (m t) -> p t m", t=4),
-                func=ACT.Identity, scale=gw32[:, t : t + 1], bias=nb[:],
+                out=ctx_rows[:, CHANNELS * t : CHANNELS * (t + 1)].rearrange("p (k m) -> p k m", k=T),
+                in_=maximum[i][:].rearrange("p (m k) -> p k m", k=T),
+                func=ACT.Identity, scale=gw_f32[:, t : t + 1], bias=bias[i][:],
             )
 
-        def ctx_interleave(b):
-            cg = two.tile([128, 4 * 512], BF16, name="cg", align_bytes=64)
-            ctxb[b, "g"] = cg
+        def pack_ctx(b):
+            ctx_packed[b] = rotating("ctx_packed", 2, [PARTS, T * CHANNELS], BF16, 64)
             nc.vector.tensor_copy(
-                out=cg[:].rearrange("p (o t) -> p o t", t=4),
-                in_=ctxb[b][:].rearrange("p (t o) -> p o t", t=4),
+                out=ctx_packed[b][:].rearrange("p (o t) -> p o t", t=T),
+                in_=ctx_rows[:].rearrange("p (t o) -> p o t", t=T),
             )
 
-        def ctx_quantize(b):
-            cq[b] = quantize(two, "cq", ctxb[b, "g"][:], 512)
+        def centre_packed(i, k):
+            b, t = divmod(i, T)
+            half = ctx_packed[b][:, 1024 * k : 1024 * (k + 1)]
+            nc.vector.tensor_scalar(
+                out=half.rearrange("p (k m t) -> p k m t", k=2, t=T)[:, :, :, t],
+                in0=maximum[i][:].rearrange("p (m k) -> p k m", k=T)[:, 2 * k : 2 * k + 2, :],
+                scalar1=gw_f32[:, t : t + 1], scalar2=bias[i][:], op0=ALU.mult, op1=ALU.add,
+            )
 
-        smx = {}
+        def quantise_ctx_halves(b):
+            codes = rotating("ctx_codes", 2, [PARTS, CHANNELS], U32, 64)
+            scale = rotating("ctx_scale", 2, [PARTS, CHANNELS], U8, 64)
+            ctx_quant[b] = (codes, scale)
+            for k in range(2):
+                c = slice(256 * k, 256 * (k + 1))
+                nc.vector.quantize_mx(
+                    out=codes[:, c].bitcast(E4M3), scales=scale[:, c],
+                    in_=ctx_packed[b][:, 1024 * k : 1024 * (k + 1)],
+                )
 
-        def sm_max(b):
-            d = dlt[b][:].rearrange("p (t n) -> p t n", t=4)
-            a1 = two.tile([128, 4, 256], BF16, name="a1", bufs=1)
-            a2 = two.tile([128, 4, 128], BF16, name="a2", bufs=1)
-            a3 = two.tile([128, 4, 64], BF16, name="a3", bufs=1)
-            mx = two.tile([128, 4], F32, name="mx")
-            nmx = two.tile([128, 4], F32, name="nmx")
-            e_t = two.tile([128, 4 * 512], F32, name="e_t")
-            es = two.tile([128, 4], F32, name="es")
-            smx[b] = (nmx, e_t, es)
+        softmax = {}
+        d_rows = {}
+        d_quant = {}
+
+        def softmax_maximum(b):
+            rows = dl_in[b][:].rearrange("p (t n) -> p t n", t=T)
+            max_256 = rotating("max_256", 1, [PARTS, T, 256], BF16)
+            max_128 = rotating("max_128", 1, [PARTS, T, 128], BF16)
+            max_64 = rotating("max_64", 1, [PARTS, T, 64], BF16)
+            top = rotating("top", 2, [PARTS, T], F32)
+            minus_top = rotating("minus_top", 2, [PARTS, T], F32)
+            exps = rotating("exps", 2, [PARTS, T * BINS], F32)
+            sums = rotating("sums", 2, [PARTS, T], F32)
+            softmax[b] = (minus_top, exps, sums)
+
+            def halve(out, rows_in, n):
+                nc.vector.tensor_tensor(
+                    out=out[:], in0=rows_in[:, :, 0:n], in1=rows_in[:, :, n : 2 * n], op=ALU.max
+                )
+
             return [
-                lambda: nc.vector.tensor_tensor(out=a1[:], in0=d[:, :, 0:256], in1=d[:, :, 256:512], op=ALU.max),
-                lambda: nc.vector.tensor_tensor(out=a2[:], in0=a1[:, :, 0:128], in1=a1[:, :, 128:256], op=ALU.max),
-                lambda: nc.vector.tensor_tensor(out=a3[:], in0=a2[:, :, 0:64], in1=a2[:, :, 64:128], op=ALU.max),
-                lambda: nc.vector.tensor_reduce(out=mx[:], in_=a3[:], axis=AX.X, op=ALU.max),
+                lambda: halve(max_256, rows, 256),
+                lambda: halve(max_128, max_256, 128),
+                lambda: halve(max_64, max_128, 64),
+                lambda: nc.vector.tensor_reduce(out=top[:], in_=max_64[:], axis=AX.X, op=ALU.max),
                 lambda: nc.vector.tensor_scalar(
-                    out=nmx[:], in0=mx[:], scalar1=-1.0, scalar2=None, op0=ALU.mult
+                    out=minus_top[:], in0=top[:], scalar1=-1.0, scalar2=None, op0=ALU.mult
                 ),
             ]
 
-        def sm_exp(b, ts):
-            nmx, e_t, es = smx[b]
-            for t in ts:
+        def exponentials(b, tiles):
+            minus_top, exps, sums = softmax[b]
+            for t in tiles:
+                c = slice(BINS * t, BINS * (t + 1))
                 nc.scalar.activation(
-                    out=e_t[:, 512 * t : 512 * (t + 1)].rearrange("p (u q e) -> p u q e", u=2, e=2),
-                    in_=dlt[b][:, 512 * t : 512 * (t + 1)].rearrange("p (q u e) -> p u q e", u=2, e=2),
-                    func=ACT.Exp, bias=nmx[:, t : t + 1], scale=1.0, accum_out=es[:, t : t + 1],
+                    out=exps[:, c].rearrange("p (u q e) -> p u q e", u=2, e=2),
+                    in_=dl_in[b][:, c].rearrange("p (q u e) -> p u q e", u=2, e=2),
+                    func=ACT.Exp, bias=minus_top[:, t : t + 1], scale=1.0, accum_out=sums[:, t : t + 1],
                 )
 
-        dg = {}
-        dxg = {}
-        dq = {}
-
-        def sm_norm(b, ts):
-            nmx, e_t, es = smx[b]
-            if 0 in ts:
-                ri = two.tile([128, 4], F32, name="ri")
-                nc.vector.reciprocal(out=ri[:], in_=es[:])
-                dgt = two.tile([128, 4 * 512], BF16, name="dgt", bufs=1)
-                dg[b] = dgt
-                smx[b, "ri"] = ri
-            for t in ts:
-                c = slice(512 * t, 512 * (t + 1))
+        def normalise(b, tiles):
+            exps, sums = softmax[b][1:3]
+            if 0 in tiles:
+                inverse = rotating("inverse", 2, [PARTS, T], F32)
+                nc.vector.reciprocal(out=inverse[:], in_=sums[:])
+                d_rows[b] = (rotating("d_rows", 1, [PARTS, T * BINS], BF16), inverse)
+            rows, inverse = d_rows[b]
+            for t in tiles:
+                c = slice(BINS * t, BINS * (t + 1))
                 nc.vector.scalar_tensor_tensor(
-                    out=dg[b][:, c], in0=e_t[:, c], scalar=smx[b, "ri"][:, t : t + 1], in1=gd512[:],
+                    out=rows[:, c], in0=exps[:, c], scalar=inverse[:, t : t + 1], in1=gd_512[:],
                     op0=ALU.mult, op1=ALU.mult,
                 )
 
-        fb = {}
+        turned_banks = {}
+        d_packed = {}
 
-        def extra_pe(unit):
-            kind, k = unit
+        def turn(kind, k):
             for a in range(2):
-                bank = ps_f.tile([128, 512], F32, name="fb")
-                fb[unit, a] = bank
-                if kind == "ray":
-                    for jj in range(2):
+                bank = unit_bank()
+                turned_banks[kind, k, a] = bank
+                for n in range(4):
+                    if kind == "ray":
+                        jj, u = divmod(n, 2)
                         j = 4 * k + 2 * a + jj
-                        words = rayin[:, 512 * j : 512 * (j + 1)].bitcast(F32)
-                        for u in range(2):
-                            c = 2 * jj + u
-                            nc.tensor.transpose(bank[:, 128 * c : 128 * (c + 1)], words[:, u:256:2], ident[:])
-                else:
-                    words = dg[k][:].bitcast(F32)
-                    for c in range(4):
-                        src = 512 * a + 128 * c
-                        nc.tensor.transpose(
-                            bank[:, 128 * c : 128 * (c + 1)], words[:, src : src + 128], ident[:]
-                        )
+                        source = ray_in[:, 512 * j : 512 * (j + 1)].bitcast(F32)[:, u:256:2]
+                    else:
+                        first = BANK * a + PARTS * n
+                        source = d_rows[k][0][:].bitcast(F32)[:, first : first + PARTS]
+                    nc.tensor.transpose(bank[:, PARTS * n : PARTS * (n + 1)], source, ident[:])
 
-        def extra_evac(unit, engs):
-            kind, k = unit
+        def empty_turned(kind, k):
             if kind == "ray":
-                w = rayg[:].bitcast(F32)
-                for a in range(2):
-                    c = 1024 * k + 512 * a
-                    copy_words(engs[a], w[:, c : c + 512], fb[unit, a][:], 2)
+                words = ray_t[:].bitcast(F32)[:, 1024 * k : 1024 * (k + 1)]
             else:
-                dx = two.tile([128, 4 * 512], BF16, name="dx", align_bytes=64, bufs=1)
-                dxg[k] = dx
-                w = dx[:].bitcast(F32)
-                for a in range(2):
-                    copy_words(engs[a], w[:, 512 * a : 512 * (a + 1)], fb[unit, a][:], 2)
+                d_packed[k] = rotating("d_packed", 1, [PARTS, T * BINS], BF16, 64)
+                words = d_packed[k][:].bitcast(F32)
+            for a in range(2):
+                copy_words("S", words[:, BANK * a : BANK * (a + 1)], turned_banks[kind, k, a][:])
 
-        tg = {}
-        tq = {}
-        pg = {}
-        pq = {}
-        ob = {}
+        unit_banks = {}
+        tm_packed = {}
+        tm_quant = {}
+        planes_packed = {}
+        planes_quant = {}
 
-        def fill_pe(unit, where=0):
+        def multiply_unit(unit, bank):
             kind, b, j = unit
-            if where == 0:
-                bank = ps_f.tile([128, 512], F32, name="fb")
-            elif where == 1:
-                bank = ps_y.tile([128, 512], F32, name="y")
-            else:
-                bank = ps_t.tile([128, 512], F32, name="xp")
-            fb[unit] = bank
-            jc = slice(128 * j, 128 * (j + 1))
+            unit_banks[unit] = bank
+            cells = slice(PARTS * j, PARTS * (j + 1))
             if kind == "o":
                 nc.tensor.matmul_mx(
                     out=bank[:],
-                    lhsT=tq[b][0][:, jc].bitcast(E4M3), lhsT_scale=tq[b][1][:, jc],
-                    rhs=cq[b][0][:].bitcast(E4M3), rhs_scale=cq[b][1][:],
+                    lhsT=tm_quant[b][0][:, cells].bitcast(E4M3), lhsT_scale=tm_quant[b][1][:, cells],
+                    rhs=ctx_quant[b][0][:].bitcast(E4M3), rhs_scale=ctx_quant[b][1][:],
                     start=True, stop=True,
                 )
                 return
-            for t in range(4):
-                c = slice(128 * t, 128 * (t + 1))
-                if kind == "tm":
-                    nc.tensor.matmul_mx(
-                        out=bank[:, c],
-                        lhsT=dq[b][0][:, c].bitcast(E4M3), lhsT_scale=dq[b][1][:, c],
-                        rhs=ringw[:, 256 * j : 256 * (j + 1)].bitcast(E2M1), rhs_scale=rings[:, 0, jc],
-                        start=True, stop=True,
-                    )
+            for t in range(T):
+                c = slice(PARTS * t, PARTS * (t + 1))
+                if kind == "t":
+                    codes, scale = d_quant[b]
+                    rhs = ring_codes[:, 256 * j : 256 * (j + 1)].bitcast(E2M1)
+                    rhs_scale = ring_scale[:, 0, cells]
                 else:
-                    nc.tensor.matmul_mx(
-                        out=bank[:, c],
-                        lhsT=cq[b][0][:, c].bitcast(E4M3), lhsT_scale=cq[b][1][:, c],
-                        rhs=tq[b][0][:, jc].bitcast(E4M3), rhs_scale=tq[b][1][:, jc],
-                        start=True, stop=True,
-                    )
+                    codes, scale = ctx_quant[b]
+                    rhs = tm_quant[b][0][:, cells].bitcast(E4M3)
+                    rhs_scale = tm_quant[b][1][:, cells]
+                nc.tensor.matmul_mx(
+                    out=bank[:, c], lhsT=codes[:, c].bitcast(E4M3), lhsT_scale=scale[:, c],
+                    rhs=rhs, rhs_scale=rhs_scale, start=True, stop=True,
+                )
 
-        def fill_evac(unit, eng):
+        def empty_unit(unit, engine):
             kind, b, j = unit
-            jj = j % 4
-            cols = slice(512 * jj, 512 * (jj + 1))
-            bank = fb[unit]
-            src = bank[:].rearrange("p (t n) -> p n t", t=4)
-            if kind == "tm":
+            group, jj = divmod(j, 4)
+            c = slice(BANK * jj, BANK * (jj + 1))
+            source = unit_banks[unit][:].rearrange("p (t n) -> p n t", t=T)
+            if kind == "t":
                 if jj == 0:
-                    tgt = two.tile([128, 4 * 512], BF16, name="tgt", align_bytes=64)
-                    tg[b, j // 4] = tgt
+                    tm_packed[b, group] = rotating("tm_packed", 2, [PARTS, 4 * BANK], BF16, 64)
                 nc.vector.tensor_tensor(
-                    out=tg[b, j // 4][:, cols].rearrange("p (n t) -> p n t", t=4),
-                    in0=src,
-                    in1=rayg[:, 512 * j : 512 * (j + 1)].rearrange("p (n t) -> p n t", t=4),
+                    out=tm_packed[b, group][:, c].rearrange("p (n t) -> p n t", t=T),
+                    in0=source,
+                    in1=ray_t[:, BANK * j : BANK * (j + 1)].rearrange("p (n t) -> p n t", t=T),
                     op=ALU.mult,
                 )
                 return
-            if kind == "pl":
+            if kind == "p":
                 if jj == 0:
-                    pgt = two.tile([128, 4 * 512], BF16, name="pgt", align_bytes=64)
-                    pg[b, j // 4] = pgt
-                dst = pg[b, j // 4][:, cols]
+                    planes_packed[b, group] = rotating("planes_packed", 2, [PARTS, 4 * BANK], BF16, 64)
+                target = planes_packed[b, group][:, c]
             else:
-                if jj == 0:
-                    obt = two.tile([128, 4 * 512], F32, name="obt")
-                    ob[b, j // 4] = obt
-                dst = ob[b, j // 4][:, cols]
-            dst = dst.rearrange("p (n t) -> p n t", t=4)
-            if eng == "S":
-                nc.scalar.copy(out=dst, in_=src)
+                result = rotating("result", 11, [PARTS, CHANNELS], F32)
+                target = result[:]
+            target_view = target.rearrange("p (n t) -> p n t", t=T)
+            if engine == "S":
+                nc.scalar.copy(out=target_view, in_=source)
             else:
-                nc.vector.tensor_copy(out=dst, in_=src)
+                nc.vector.tensor_copy(out=target_view, in_=source)
             if kind == "o":
-                nc.sync.dma_start(out=out_0[b, 128 * j : 128 * (j + 1), :], in_=ob[b, j // 4][:, cols])
+                nc.sync.dma_start(out=out_0[b, PARTS * j : PARTS * (j + 1), :], in_=target)
 
-        def fill_quantize(unit):
+        def quantise_group(unit):
             kind, b, j = unit
-            if kind == "o" or j % 4 != 3:
+            group, jj = divmod(j, 4)
+            if kind == "o" or jj != 3:
                 return
-            h = j // 4
-            c = slice(512 * h, 512 * (h + 1))
-            store, group, tag = (tq, tg, "tq") if kind == "tm" else (pq, pg, "pq")
-            if h == 0:
-                codes = two.tile([128, 1024], U32, name=tag + "c", align_bytes=64)
-                scales = two.tile([128, 1024], U8, name=tag + "s", align_bytes=64)
-                store[b] = (codes, scales)
-            codes, scales = store[b]
-            nc.vector.quantize_mx(out=codes[:, c].bitcast(E4M3), scales=scales[:, c], in_=group[b, h][:])
-            if kind == "pl":
-                m0 = 1024 * b + 512 * h
+            c = slice(512 * group, 512 * (group + 1))
+            quant, packed, tag = (tm_quant, tm_packed, "tm") if kind == "t" else (planes_quant, planes_packed, "planes")
+            if group == 0:
+                quant[b] = (
+                    rotating(tag + "_codes", 2, [PARTS, CELLS], U32, 64),
+                    rotating(tag + "_scale", 2, [PARTS, CELLS], U8, 64),
+                )
+            codes, scale = quant[b]
+            nc.vector.quantize_mx(out=codes[:, c].bitcast(E4M3), scales=scale[:, c], in_=packed[b, group][:])
+            if kind == "p":
+                first = CELLS * b + 512 * group
                 nc.sync.dma_start(
-                    out=out_1[0].rearrange("p m t -> p (m t)")[:, 4 * m0 : 4 * m0 + 2048].bitcast(I32),
+                    out=out_1[0].rearrange("p m t -> p (m t)")[:, 4 * first : 4 * (first + 512)].bitcast(I32),
                     in_=codes[:, c].bitcast(I32),
                 )
-                if h == 1:
+                if group == 1:
                     for q in range(4):
                         nc.sync.dma_start(
-                            out=out_2[0, 4 * q : 4 * q + 4, 1024 * b : 1024 * (b + 1)].bitcast(I32),
-                            in_=scales[32 * q : 32 * q + 4, :].bitcast(I32),
+                            out=out_2[0, 4 * q : 4 * q + 4, CELLS * b : CELLS * (b + 1)].bitcast(I32),
+                            in_=scale[32 * q : 32 * q + 4, :].bitcast(I32),
                         )
 
-        x_transposes(0)
-        x_copies(0, "SV")
-        x_quantize(0)
-        x_transposes(1)
-        gdp = ps_f.tile([128, 512], F32, name="fb")
-        nc.tensor.matmul(gdp[:], ones[:], gz[:], start=True, stop=True)
+        turn_x(0)
+        gd_bank = unit_bank()
+        nc.tensor.matmul(gd_bank[:], ones[:], gd_row[:], start=True, stop=True)
+        nc.scalar.activation(
+            out=gd_512[:].rearrange("p (u q e) -> p u q e", u=2, e=2),
+            in_=gd_bank[:].rearrange("p (q u e) -> p u q e", u=2, e=2),
+            func=ACT.Copy, scale=float(BINS),
+        )
+        for call in softmax_maximum(0):
+            call()
+        copy_x(0, "V")
+        turn_x(1)
+        quantise_x(0)
+        exponentials(0, range(T))
 
-        last = []
-        last_x = []
+        counts = {"t": 0, "p": 0, "o": 0}
+        waiting = []
         for s in range(STEPS):
             i, half = divmod(s, 2)
-            v_evac = [u for u in last if u[0] == "tm" or u in PLAN["vec"]]
-            s_evac = [u for u in last if u not in v_evac]
-            y_matmuls(s)
-            for tok in PLAN["S"][half]:
-                if tok == "C" and s + 1 < STEPS:
-                    x_copies(s + 1, "SV" if s == 0 else "SS")
-                if tok == "x":
-                    for unit in last_x:
-                        extra_evac(unit, PLAN["xe"].get(unit, "SS"))
-                if tok == "y" and half == 0:
-                    max_first(s)
-                if tok == "y" and s == 0:
-                    nc.scalar.activation(
-                        out=gd512[:].rearrange("p (u q e) -> p u q e", u=2, e=2),
-                        in_=gdp[:].rearrange("p (q u e) -> p u q e", u=2, e=2),
-                        func=ACT.Copy, scale=512.0,
-                    )
-                if tok == "e":
-                    for unit in s_evac[:1]:
-                        fill_evac(unit, "S")
-                    s_evac = s_evac[1:]
-                if tok == "E":
-                    for unit in s_evac:
-                        fill_evac(unit, "S")
-                    s_evac = []
-                if tok == "b" and half == 0 and s > 0:
-                    centre_bias(i - 1)
-                if tok == "c" and half == 0 and s > 0:
-                    centre(i - 1)
-                if tok == "X" and s in PLAN["exp"]:
-                    sm_exp(*PLAN["exp"][s])
-            todo = []
-            if s in PLAN["max"]:
-                todo = sm_max(PLAN["max"][s])
+            on_vector = [u for u in waiting if u[0] == "t"]
+            on_scalar = [u for u in waiting if u[0] != "t"]
+            turned = TURNED.get(s - 1)
+            small = []
+            if s == 0:
+                small = softmax_maximum(1)
             if s == 1:
-                todo = [
-                    lambda: nc.vector.tensor_copy(out=gw32[:], in_=gwb[:]),
-                    lambda: nc.vector.tensor_scalar(out=gwn[:], in0=gw32[:], scalar1=-1.0 / 512.0, scalar2=None, op0=ALU.mult),
+                small = [
+                    lambda: nc.vector.tensor_copy(out=gw_f32[:], in_=gw_bf16[:]),
+                    lambda: nc.vector.tensor_scalar(
+                        out=gw_mean[:], in0=gw_f32[:], scalar1=-1.0 / CHANNELS, scalar2=None, op0=ALU.mult
+                    ),
                 ]
-            for tok in PLAN["V"][half] + "MMMMM":
-                if tok == "Q" and s + 1 < STEPS:
-                    x_quantize(s + 1)
-                if tok == "A" and half == 1:
-                    max_first(s)
-                if tok == "B":
-                    max_second(s)
-                if tok == "e":
-                    for unit in v_evac[:1]:
-                        fill_evac(unit, "V")
-                    v_evac = v_evac[1:]
-                if tok == "E":
-                    for unit in v_evac:
-                        fill_evac(unit, "V")
-                    v_evac = []
-                if tok == "D":
-                    for unit in last_x:
-                        if unit[0] == "d":
-                            dq[unit[1]] = quantize(two, "dq", dxg[unit[1]][:], 512)
-                if tok == "I" and s == PLAN["ctx"]:
-                    ctx_interleave(0)
-                if tok == "G":
-                    for unit in last:
-                        fill_quantize(unit)
-                if tok == "K" and s == PLAN["ctx"]:
-                    ctx_quantize(0)
-                if tok == "M":
-                    if todo:
-                        todo.pop(0)()
-                if tok == "N":
-                    for b_t in PLAN["norm"].get(s, []):
-                        sm_norm(*b_t)
-            for unit in PLAN["fill"].get(s, []):
-                fill_pe(unit)
-            if s + 2 < STEPS:
-                x_transposes(s + 2)
-            for unit in PLAN["extra"].get(s, []):
-                extra_pe(unit)
-            last = PLAN["fill"].get(s, [])
-            last_x = PLAN["extra"].get(s, [])
 
-        rest = PLAN["rest"]
+            multiply_y(s)
+
+            for work in (SCALAR_EARLY if s < EARLY else SCALAR_LATE)[half]:
+                if work == "copy x" and s + 1 < STEPS:
+                    copy_x(s + 1, "V" if s == 0 else "S")
+                elif work == "sort x":
+                    sort_x(s + 3)
+                elif work == "height 0":
+                    height_zero(i)
+                elif work == "bias" and s > 0:
+                    centre_bias(i - 1)
+                elif work == "centre" and s > 0:
+                    centre(i - 1)
+                elif work == "exponential":
+                    exponentials(1, EXPONENTIALS[s])
+                elif work == "empty turned" and turned is not None:
+                    empty_turned(*turned)
+                elif work == "empty one" or work == "empty rest":
+                    count = 1 if work == "empty one" else len(on_scalar)
+                    for unit in on_scalar[:count]:
+                        empty_unit(unit, "S")
+                    on_scalar = on_scalar[count:]
+
+            for work in (VECTOR_EARLY if s < EARLY else VECTOR_LATE)[half]:
+                if work == "quantise x" and s + 1 < STEPS:
+                    quantise_x(s + 1)
+                elif work == "first height":
+                    next_height(i, s, 0)
+                elif work == "second height":
+                    if half == 0:
+                        next_height(i, s, 1)
+                    else:
+                        last_height(i, s)
+                elif work == "small" and small:
+                    small.pop(0)()
+                elif work == "normalise" and s in NORMALISED:
+                    normalise(*NORMALISED[s])
+                elif work == "quantise d" and turned is not None and turned[0] == "d":
+                    d_quant[turned[1]] = quantise("d", 2, d_packed[turned[1]][:], 512)
+                elif work == "pack ctx" and s == CTX_STEP:
+                    pack_ctx(0)
+                elif work == "pack ctx" and s == STEPS - 1:
+                    pack_ctx(1)
+                elif work == "quantise ctx" and s == CTX_STEP:
+                    ctx_quant[0] = quantise("ctx", 2, ctx_packed[0][:], CHANNELS)
+                elif work == "empty one" or work == "empty rest":
+                    count = 1 if work == "empty one" else len(on_vector)
+                    for unit in on_vector[:count]:
+                        empty_unit(unit, "V")
+                    on_vector = on_vector[count:]
+                elif work == "quantise group":
+                    for unit in waiting:
+                        quantise_group(unit)
+
+            waiting = unit_list(UNITS.get(s, ""), counts)
+            for unit in waiting:
+                multiply_unit(unit, unit_bank())
+            if s + 2 < STEPS:
+                turn_x(s + 2)
+            if s in TURNED:
+                turn(*TURNED[s])
+
         centre_bias(7)
-        centre(7)
-        for n, unit in enumerate(rest):
-            fill_pe(unit, (1, 2)[n % 2])
-        for unit in last + rest:
-            fill_evac(unit, "S")
-        ctx_interleave(1)
-        ctx_quantize(1)
-        order = []
-        for j in range(8):
-            order += [("pl", 1, j), ("o", 1, j)]
-        waiting = []
-        for n, unit in enumerate(order):
-            fill_pe(unit, (0, 1, 0, 2)[n % 4])
-            fill_evac(unit, PLAN["tail"][n % len(PLAN["tail"])])
-            for u in waiting:
-                fill_quantize(u)
-            waiting = [unit]
-        for u in waiting:
-            fill_quantize(u)
+        centre_packed(7, 0)
+        centre_packed(7, 1)
+        left_over = unit_list(LEFT_OVER, counts)
+        for n, unit in enumerate(left_over):
+            multiply_unit(unit, turn_bank() if n % 2 else y_bank())
+        for unit in waiting + left_over:
+            empty_unit(unit, "S")
+        quantise_ctx_halves(1)
+        for unit in waiting:
+            quantise_group(unit)
+        banks = (unit_bank, y_bank, unit_bank, turn_bank)
+        before = []
+        for n, unit in enumerate(unit_list(LAST_UNITS, counts)):
+            multiply_unit(unit, banks[n % 4]())
+            empty_unit(unit, LAST_ENGINES[n])
+            for done in before:
+                quantise_group(done)
+            before = [unit]
+        for done in before:
+            quantise_group(done)

from contextlib import ExitStack

import concourse.mybir as mybir
from concourse.masks import make_identity

F32 = mybir.dt.float32
BF16 = mybir.dt.bfloat16
I32 = mybir.dt.int32
U32 = mybir.dt.uint32
U8 = mybir.dt.uint8
E4M3 = mybir.dt.float8_e4m3fn_x4
E2M1 = mybir.dt.float4_e2m1fn_x4
ALU = mybir.AluOpType
ACT = mybir.ActivationFunctionType
AX = mybir.AxisListType

BATCH, HEIGHTS, COLUMNS, FEATURES, BINS, CELLS, CHANNELS = 2, 4, 512, 1024, 512, 1024, 512
FLOPS = 2 * BATCH * (HEIGHTS * COLUMNS * FEATURES * CHANNELS + CELLS * BINS * COLUMNS + CELLS * COLUMNS * CHANNELS)

PARTS = 128
BANK = 512
T = 4

STEPS = BATCH * T * 2
EARLY = 4

TURNED = {0: ("ray", 0), 2: ("d", 0), 4: ("ray", 1), 6: ("d", 1)}
EXPONENTIALS = {1: (0, 1), 3: (2, 3)}
NORMALISED = {1: (0, (0, 1)), 2: (0, (2, 3)), 3: (1, (0, 1)), 6: (1, (2, 3))}
CTX_STEP = 9
UNITS = {
    4: "tt", 5: "tt", 6: "t", 7: "t", 8: "t", 9: "tt", 10: "ptp", 11: "tptp",
    12: "pto", 13: "oto", 14: "pppo", 15: "tot",
}
LEFT_OVER = "ooo"
LAST_UNITS = "pooopooopopopppp"
LAST_ENGINES = "VSSVSVSSVSVSSVSV"
SORTED_STEPS = range(8, 15)

SCALAR_EARLY = (
    ("bias", "copy x", "height 0", "centre"),
    ("copy x", "empty turned", "exponential"),
)
SCALAR_LATE = (
    ("empty one", "sort x", "empty rest", "copy x", "bias", "height 0", "centre"),
    ("empty one", "copy x", "empty rest", "empty turned", "sort x"),
)
VECTOR_EARLY = (
    ("normalise", "small", "small", "small", "quantise x", "small", "second height", "small"),
    ("small", "small", "first height", "quantise x", "second height", "quantise d", "normalise"),
)
VECTOR_LATE = (
    ("empty one", "empty rest", "normalise", "quantise x", "second height", "quantise group"),
    (
        "empty one", "pack ctx", "empty rest", "first height", "quantise group", "quantise x",
        "second height", "quantise ctx", "quantise d",
    ),
)


def unit_list(letters, counts):
    units = []
    for letter in letters:
        n = counts[letter]
        counts[letter] = n + 1
        units.append((letter, n // 8, n % 8))
    return units


def tile_matrixvtringraybev_x2_kernel(
    tc, x, wc_words, wc_scales, gw, dl, gd, ring_words, ring_scales, ray, out_0, out_1, out_2
):
    nc = tc.nc
    with ExitStack() as stack:
        pool = stack.enter_context(tc.tile_pool(name="sbuf", bufs=1))
        psum = stack.enter_context(tc.psum_pool(name="psum", bufs=1))
        stack.enter_context(tc.manual_schedule())

        made = {}

        def rotating(name, count, shape, dtype, align=None):
            n = made.get(name, 0)
            made[name] = n + 1
            if align is None:
                tile = pool.tile(shape, dtype, name="%s%d" % (name, n % count))
            else:
                tile = pool.tile(shape, dtype, name="%s%d" % (name, n % count), align_bytes=align)
            return tile

        def bank_of(name, count):
            n = made.get(name, 0)
            made[name] = n + 1
            bank = psum.tile([PARTS, BANK], F32, name="%s%d" % (name, n % count))
            return bank

        def turn_bank():
            return bank_of("turn", 2)

        def y_bank():
            return bank_of("y", 2)

        def unit_bank():
            return bank_of("unit", 4)

        ident = pool.tile([PARTS, PARTS], F32, name="ident")
        make_identity(nc, ident[:])
        wc_codes = pool.tile([PARTS, 2 * 1024], U8, name="wc_codes", align_bytes=64)
        wc_scale = pool.tile([PARTS, 2, 512], U8, name="wc_scale", align_bytes=64)
        ring_codes = pool.tile([PARTS, 2048], U8, name="ring_codes", align_bytes=64)
        ring_scale = pool.tile([PARTS, 1, 1024], U8, name="ring_scale", align_bytes=64)
        gd_row = pool.tile([PARTS, BINS], BF16, name="gd_row")
        ones = pool.tile([PARTS, PARTS], BF16, name="ones")
        gd_512 = pool.tile([PARTS, BINS], F32, name="gd_512")
        gw_bf16 = pool.tile([PARTS, T], BF16, name="gw_bf16")
        gw_f32 = pool.tile([PARTS, T], F32, name="gw_f32")
        gw_mean = pool.tile([PARTS, T], F32, name="gw_mean")
        ray_in = pool.tile([PARTS, 8 * 512], BF16, name="ray_in")
        ray_t = pool.tile([PARTS, 8 * 512], BF16, name="ray_t")
        ctx_rows = pool.tile([PARTS, T * CHANNELS], BF16, name="ctx_rows")

        nc.vector.memset(wc_scale[:].bitcast(U32), 0)
        nc.vector.memset(gd_row[:], 0.0)
        nc.vector.memset(ones[:], 1.0)
        nc.vector.memset(ring_scale[:].bitcast(U32), 0)

        x_in = {}
        dl_in = {}

        def load_x(i, h0, count):
            b, t = divmod(i, T)
            if i not in x_in:
                x_in[i] = rotating("x_in", 6, [PARTS, HEIGHTS * FEATURES], BF16)
            nc.sync.dma_start(
                out=x_in[i][:, FEATURES * h0 : FEATURES * (h0 + count)].rearrange("m (h c) -> m h c", h=count),
                in_=x[b, h0 : h0 + count, :, :].rearrange("h (m t) c -> t m h c", t=T)[t],
            )

        def load_dl(b):
            dl_in[b] = rotating("dl_in", 2, [PARTS, T * BINS], BF16)
            nc.sync.dma_start(
                out=dl_in[b][:].rearrange("m (t n) -> m t n", t=T),
                in_=dl[b].rearrange("(m t) n -> m t n", t=T),
            )

        def load_ray(half):
            nc.sync.dma_start(
                out=ray_in[:, 2048 * half : 2048 * (half + 1)].rearrange("p (j w) -> p j w", j=4),
                in_=ray[512 * half : 512 * (half + 1), :].rearrange("(j p) w -> p j w", p=PARTS),
            )

        def load_scales(engine, scale, rows):
            for q in range(4):
                engine.dma_start(
                    out=scale[32 * q : 32 * q + 4, :, :].bitcast(I32),
                    in_=rows.bitcast(I32)[:, 4 * q : 4 * q + 4, :].rearrange("g q n -> q g n"),
                )

        load_scales(nc.scalar, wc_scale, wc_scales)
        load_x(0, 0, 1)
        load_dl(0)
        load_x(0, 1, 1)
        load_x(0, 2, 2)
        nc.sync.dma_start(out=gd_row[0:1, :], in_=gd.unsqueeze(0))
        nc.sync.dma_start(
            out=wc_codes[:].bitcast(I32).rearrange("p (g n) -> p g n", g=2),
            in_=wc_words.bitcast(I32).rearrange("g p n -> p g n"),
        )
        load_x(1, 0, 2)
        load_dl(1)
        load_x(1, 2, 2)
        nc.sync.dma_start(out=gw_bf16[:], in_=gw.rearrange("(m t) -> m t", t=T))
        load_ray(0)
        nc.sync.dma_start(out=ring_codes[:].bitcast(I32), in_=ring_words[0].bitcast(I32))
        load_scales(nc.sync, ring_scale, ring_scales)
        load_x(2, 0, 4)
        load_ray(1)
        for i in range(3, 8):
            load_x(i, 0, 4)

        def quantise(tag, count, rows, columns):
            codes = rotating(tag + "_codes", count, [PARTS, columns], U32, 64)
            scale = rotating(tag + "_scale", count, [PARTS, columns], U8, 64)
            nc.vector.quantize_mx(out=codes[:].bitcast(E4M3), scales=scale[:], in_=rows)
            return codes, scale

        def copy_words(engine, out, bank):
            source = bank.rearrange("p (a u r) -> p a r u", a=2, u=2)
            target = out.rearrange("p (a r u) -> p a r u", a=2, u=2)
            if engine == "S":
                nc.scalar.copy(out=target, in_=source)
            else:
                nc.vector.tensor_copy(out=target, in_=source)

        x_sorted = {}
        x_banks = {}
        x_packed = {}
        x_quant = {}
        y_banks = {}

        def x_words(s, hh):
            i, half = divmod(s, 2)
            h = 2 * half + hh
            return x_in[i][:, FEATURES * h : FEATURES * (h + 1)].bitcast(F32)

        def sort_x(s):
            if s in SORTED_STEPS:
                x_sorted[s] = rotating("x_sorted", 3, [PARTS, FEATURES], BF16)
                nc.scalar.copy(
                    out=x_sorted[s][:].bitcast(F32).rearrange("p (g u r) -> p g u r", g=2, u=2),
                    in_=x_words(s, 1).rearrange("p (g r u) -> p g u r", g=2, u=2),
                )

        def turn_x(s):
            for hh in range(2):
                bank = turn_bank()
                x_banks[s, hh] = bank
                for n in range(4):
                    g, u = divmod(n, 2)
                    if hh == 1 and s in x_sorted:
                        source = x_sorted[s][:].bitcast(F32)[:, PARTS * n : PARTS * (n + 1)]
                    else:
                        source = x_words(s, hh)[:, 256 * g + u : 256 * (g + 1) : 2]
                    nc.tensor.transpose(bank[:, PARTS * n : PARTS * (n + 1)], source, ident[:])

        def copy_x(s, engine):
            x_packed[s] = rotating("x_packed", 4, [PARTS, 2 * FEATURES], BF16, 64)
            words = x_packed[s][:].bitcast(F32)
            for hh in range(2):
                copy_words(engine, words[:, BANK * hh : BANK * (hh + 1)], x_banks[s, hh][:])

        def quantise_x(s):
            x_quant[s] = quantise("x", 3, x_packed[s][:], 512)

        def multiply_y(s):
            codes, scale = x_quant[s]
            for hh in range(2):
                bank = y_bank()
                y_banks[s, hh] = bank
                for g in range(2):
                    c = slice(256 * hh + PARTS * g, 256 * hh + PARTS * (g + 1))
                    nc.tensor.matmul_mx(
                        out=bank[:],
                        lhsT=codes[:, c].bitcast(E4M3), lhsT_scale=scale[:, c],
                        rhs=wc_codes[:, 1024 * g : 1024 * (g + 1)].bitcast(E2M1), rhs_scale=wc_scale[:, g, :],
                        start=(g == 0), stop=(g == 1),
                    )

        maximum = {}
        channel_sum = {}
        bias = {}
        ctx_packed = {}
        ctx_quant = {}

        def height_zero(i):
            maximum[i] = rotating("maximum", 3, [PARTS, CHANNELS], F32)
            nc.scalar.copy(out=maximum[i][:], in_=y_banks[2 * i, 0][:])

        def next_height(i, s, hh):
            nc.vector.tensor_tensor(out=maximum[i][:], in0=y_banks[s, hh][:], in1=maximum[i][:], op=ALU.max)

        def last_height(i, s):
            channel_sum[i] = rotating("channel_sum", 3, [PARTS, 1], F32)
            nc.vector.scalar_tensor_tensor(
                out=maximum[i][:], in0=y_banks[s, 1][:], scalar=1.0, in1=maximum[i][:],
                op0=ALU.mult, op1=ALU.max, accum_out=channel_sum[i][:],
            )

        def centre_bias(i):
            t = i % T
            bias[i] = rotating("bias", 3, [PARTS, 1], F32)
            nc.scalar.activation(
                out=bias[i][:], in_=channel_sum[i][:], func=ACT.Copy, scale=gw_mean[:, t : t + 1]
            )

        def centre(i):
            t = i % T
            nc.scalar.activation(
                out=ctx_rows[:, CHANNELS * t : CHANNELS * (t + 1)].rearrange("p (k m) -> p k m", k=T),
                in_=maximum[i][:].rearrange("p (m k) -> p k m", k=T),
                func=ACT.Identity, scale=gw_f32[:, t : t + 1], bias=bias[i][:],
            )

        def pack_ctx(b):
            ctx_packed[b] = rotating("ctx_packed", 2, [PARTS, T * CHANNELS], BF16, 64)
            nc.vector.tensor_copy(
                out=ctx_packed[b][:].rearrange("p (o t) -> p o t", t=T),
                in_=ctx_rows[:].rearrange("p (t o) -> p o t", t=T),
            )

        def centre_packed(i, k):
            b, t = divmod(i, T)
            half = ctx_packed[b][:, 1024 * k : 1024 * (k + 1)]
            nc.vector.tensor_scalar(
                out=half.rearrange("p (k m t) -> p k m t", k=2, t=T)[:, :, :, t],
                in0=maximum[i][:].rearrange("p (m k) -> p k m", k=T)[:, 2 * k : 2 * k + 2, :],
                scalar1=gw_f32[:, t : t + 1], scalar2=bias[i][:], op0=ALU.mult, op1=ALU.add,
            )

        def quantise_ctx_halves(b):
            codes = rotating("ctx_codes", 2, [PARTS, CHANNELS], U32, 64)
            scale = rotating("ctx_scale", 2, [PARTS, CHANNELS], U8, 64)
            ctx_quant[b] = (codes, scale)
            for k in range(2):
                c = slice(256 * k, 256 * (k + 1))
                nc.vector.quantize_mx(
                    out=codes[:, c].bitcast(E4M3), scales=scale[:, c],
                    in_=ctx_packed[b][:, 1024 * k : 1024 * (k + 1)],
                )

        softmax = {}
        d_rows = {}
        d_quant = {}

        def softmax_maximum(b):
            rows = dl_in[b][:].rearrange("p (t n) -> p t n", t=T)
            max_256 = rotating("max_256", 1, [PARTS, T, 256], BF16)
            max_128 = rotating("max_128", 1, [PARTS, T, 128], BF16)
            max_64 = rotating("max_64", 1, [PARTS, T, 64], BF16)
            top = rotating("top", 2, [PARTS, T], F32)
            minus_top = rotating("minus_top", 2, [PARTS, T], F32)
            exps = rotating("exps", 2, [PARTS, T * BINS], F32)
            sums = rotating("sums", 2, [PARTS, T], F32)
            softmax[b] = (minus_top, exps, sums)

            def halve(out, rows_in, n):
                nc.vector.tensor_tensor(
                    out=out[:], in0=rows_in[:, :, 0:n], in1=rows_in[:, :, n : 2 * n], op=ALU.max
                )

            return [
                lambda: halve(max_256, rows, 256),
                lambda: halve(max_128, max_256, 128),
                lambda: halve(max_64, max_128, 64),
                lambda: nc.vector.tensor_reduce(out=top[:], in_=max_64[:], axis=AX.X, op=ALU.max),
                lambda: nc.vector.tensor_scalar(
                    out=minus_top[:], in0=top[:], scalar1=-1.0, scalar2=None, op0=ALU.mult
                ),
            ]

        def exponentials(b, tiles):
            minus_top, exps, sums = softmax[b]
            for t in tiles:
                c = slice(BINS * t, BINS * (t + 1))
                nc.scalar.activation(
                    out=exps[:, c].rearrange("p (u q e) -> p u q e", u=2, e=2),
                    in_=dl_in[b][:, c].rearrange("p (q u e) -> p u q e", u=2, e=2),
                    func=ACT.Exp, bias=minus_top[:, t : t + 1], scale=1.0, accum_out=sums[:, t : t + 1],
                )

        def normalise(b, tiles):
            exps, sums = softmax[b][1:3]
            if 0 in tiles:
                inverse = rotating("inverse", 2, [PARTS, T], F32)
                nc.vector.reciprocal(out=inverse[:], in_=sums[:])
                d_rows[b] = (rotating("d_rows", 1, [PARTS, T * BINS], BF16), inverse)
            rows, inverse = d_rows[b]
            for t in tiles:
                c = slice(BINS * t, BINS * (t + 1))
                nc.vector.scalar_tensor_tensor(
                    out=rows[:, c], in0=exps[:, c], scalar=inverse[:, t : t + 1], in1=gd_512[:],
                    op0=ALU.mult, op1=ALU.mult,
                )

        turned_banks = {}
        d_packed = {}

        def turn(kind, k):
            for a in range(2):
                bank = unit_bank()
                turned_banks[kind, k, a] = bank
                for n in range(4):
                    if kind == "ray":
                        jj, u = divmod(n, 2)
                        j = 4 * k + 2 * a + jj
                        source = ray_in[:, 512 * j : 512 * (j + 1)].bitcast(F32)[:, u:256:2]
                    else:
                        first = BANK * a + PARTS * n
                        source = d_rows[k][0][:].bitcast(F32)[:, first : first + PARTS]
                    nc.tensor.transpose(bank[:, PARTS * n : PARTS * (n + 1)], source, ident[:])

        def empty_turned(kind, k):
            if kind == "ray":
                words = ray_t[:].bitcast(F32)[:, 1024 * k : 1024 * (k + 1)]
            else:
                d_packed[k] = rotating("d_packed", 1, [PARTS, T * BINS], BF16, 64)
                words = d_packed[k][:].bitcast(F32)
            for a in range(2):
                copy_words("S", words[:, BANK * a : BANK * (a + 1)], turned_banks[kind, k, a][:])

        unit_banks = {}
        tm_packed = {}
        tm_quant = {}
        planes_packed = {}
        planes_quant = {}

        def multiply_unit(unit, bank):
            kind, b, j = unit
            unit_banks[unit] = bank
            cells = slice(PARTS * j, PARTS * (j + 1))
            if kind == "o":
                nc.tensor.matmul_mx(
                    out=bank[:],
                    lhsT=tm_quant[b][0][:, cells].bitcast(E4M3), lhsT_scale=tm_quant[b][1][:, cells],
                    rhs=ctx_quant[b][0][:].bitcast(E4M3), rhs_scale=ctx_quant[b][1][:],
                    start=True, stop=True,
                )
                return
            for t in range(T):
                c = slice(PARTS * t, PARTS * (t + 1))
                if kind == "t":
                    codes, scale = d_quant[b]
                    rhs = ring_codes[:, 256 * j : 256 * (j + 1)].bitcast(E2M1)
                    rhs_scale = ring_scale[:, 0, cells]
                else:
                    codes, scale = ctx_quant[b]
                    rhs = tm_quant[b][0][:, cells].bitcast(E4M3)
                    rhs_scale = tm_quant[b][1][:, cells]
                nc.tensor.matmul_mx(
                    out=bank[:, c], lhsT=codes[:, c].bitcast(E4M3), lhsT_scale=scale[:, c],
                    rhs=rhs, rhs_scale=rhs_scale, start=True, stop=True,
                )

        def empty_unit(unit, engine):
            kind, b, j = unit
            group, jj = divmod(j, 4)
            c = slice(BANK * jj, BANK * (jj + 1))
            source = unit_banks[unit][:].rearrange("p (t n) -> p n t", t=T)
            if kind == "t":
                if jj == 0:
                    tm_packed[b, group] = rotating("tm_packed", 2, [PARTS, 4 * BANK], BF16, 64)
                nc.vector.tensor_tensor(
                    out=tm_packed[b, group][:, c].rearrange("p (n t) -> p n t", t=T),
                    in0=source,
                    in1=ray_t[:, BANK * j : BANK * (j + 1)].rearrange("p (n t) -> p n t", t=T),
                    op=ALU.mult,
                )
                return
            if kind == "p":
                if jj == 0:
                    planes_packed[b, group] = rotating("planes_packed", 2, [PARTS, 4 * BANK], BF16, 64)
                target = planes_packed[b, group][:, c]
            else:
                result = rotating("result", 11, [PARTS, CHANNELS], F32)
                target = result[:]
            target_view = target.rearrange("p (n t) -> p n t", t=T)
            if engine == "S":
                nc.scalar.copy(out=target_view, in_=source)
            else:
                nc.vector.tensor_copy(out=target_view, in_=source)
            if kind == "o":
                nc.sync.dma_start(out=out_0[b, PARTS * j : PARTS * (j + 1), :], in_=target)

        def quantise_group(unit):
            kind, b, j = unit
            group, jj = divmod(j, 4)
            if kind == "o" or jj != 3:
                return
            c = slice(512 * group, 512 * (group + 1))
            quant, packed, tag = (tm_quant, tm_packed, "tm") if kind == "t" else (planes_quant, planes_packed, "planes")
            if group == 0:
                quant[b] = (
                    rotating(tag + "_codes", 2, [PARTS, CELLS], U32, 64),
                    rotating(tag + "_scale", 2, [PARTS, CELLS], U8, 64),
                )
            codes, scale = quant[b]
            nc.vector.quantize_mx(out=codes[:, c].bitcast(E4M3), scales=scale[:, c], in_=packed[b, group][:])
            if kind == "p":
                first = CELLS * b + 512 * group
                nc.sync.dma_start(
                    out=out_1[0].rearrange("p m t -> p (m t)")[:, 4 * first : 4 * (first + 512)].bitcast(I32),
                    in_=codes[:, c].bitcast(I32),
                )
                if group == 1:
                    for q in range(4):
                        nc.sync.dma_start(
                            out=out_2[0, 4 * q : 4 * q + 4, CELLS * b : CELLS * (b + 1)].bitcast(I32),
                            in_=scale[32 * q : 32 * q + 4, :].bitcast(I32),
                        )

        turn_x(0)
        gd_bank = unit_bank()
        nc.tensor.matmul(gd_bank[:], ones[:], gd_row[:], start=True, stop=True)
        nc.scalar.activation(
            out=gd_512[:].rearrange("p (u q e) -> p u q e", u=2, e=2),
            in_=gd_bank[:].rearrange("p (q u e) -> p u q e", u=2, e=2),
            func=ACT.Copy, scale=float(BINS),
        )
        for call in softmax_maximum(0):
            call()
        copy_x(0, "V")
        turn_x(1)
        quantise_x(0)
        exponentials(0, range(T))

        counts = {"t": 0, "p": 0, "o": 0}
        waiting = []
        for s in range(STEPS):
            i, half = divmod(s, 2)
            on_vector = [u for u in waiting if u[0] == "t"]
            on_scalar = [u for u in waiting if u[0] != "t"]
            turned = TURNED.get(s - 1)
            small = []
            if s == 0:
                small = softmax_maximum(1)
            if s == 1:
                small = [
                    lambda: nc.vector.tensor_copy(out=gw_f32[:], in_=gw_bf16[:]),
                    lambda: nc.vector.tensor_scalar(
                        out=gw_mean[:], in0=gw_f32[:], scalar1=-1.0 / CHANNELS, scalar2=None, op0=ALU.mult
                    ),
                ]

            multiply_y(s)

            for work in (SCALAR_EARLY if s < EARLY else SCALAR_LATE)[half]:
                if work == "copy x" and s + 1 < STEPS:
                    copy_x(s + 1, "V" if s == 0 else "S")
                elif work == "sort x":
                    sort_x(s + 3)
                elif work == "height 0":
                    height_zero(i)
                elif work == "bias" and s > 0:
                    centre_bias(i - 1)
                elif work == "centre" and s > 0:
                    centre(i - 1)
                elif work == "exponential":
                    exponentials(1, EXPONENTIALS[s])
                elif work == "empty turned" and turned is not None:
                    empty_turned(*turned)
                elif work == "empty one" or work == "empty rest":
                    count = 1 if work == "empty one" else len(on_scalar)
                    for unit in on_scalar[:count]:
                        empty_unit(unit, "S")
                    on_scalar = on_scalar[count:]

            for work in (VECTOR_EARLY if s < EARLY else VECTOR_LATE)[half]:
                if work == "quantise x" and s + 1 < STEPS:
                    quantise_x(s + 1)
                elif work == "first height":
                    next_height(i, s, 0)
                elif work == "second height":
                    if half == 0:
                        next_height(i, s, 1)
                    else:
                        last_height(i, s)
                elif work == "small" and small:
                    small.pop(0)()
                elif work == "normalise" and s in NORMALISED:
                    normalise(*NORMALISED[s])
                elif work == "quantise d" and turned is not None and turned[0] == "d":
                    d_quant[turned[1]] = quantise("d", 2, d_packed[turned[1]][:], 512)
                elif work == "pack ctx" and s == CTX_STEP:
                    pack_ctx(0)
                elif work == "pack ctx" and s == STEPS - 1:
                    pack_ctx(1)
                elif work == "quantise ctx" and s == CTX_STEP:
                    ctx_quant[0] = quantise("ctx", 2, ctx_packed[0][:], CHANNELS)
                elif work == "empty one" or work == "empty rest":
                    count = 1 if work == "empty one" else len(on_vector)
                    for unit in on_vector[:count]:
                        empty_unit(unit, "V")
                    on_vector = on_vector[count:]
                elif work == "quantise group":
                    for unit in waiting:
                        quantise_group(unit)

            waiting = unit_list(UNITS.get(s, ""), counts)
            for unit in waiting:
                multiply_unit(unit, unit_bank())
            if s + 2 < STEPS:
                turn_x(s + 2)
            if s in TURNED:
                turn(*TURNED[s])

        centre_bias(7)
        centre_packed(7, 0)
        centre_packed(7, 1)
        left_over = unit_list(LEFT_OVER, counts)
        for n, unit in enumerate(left_over):
            multiply_unit(unit, turn_bank() if n % 2 else y_bank())
        for unit in waiting + left_over:
            empty_unit(unit, "S")
        quantise_ctx_halves(1)
        for unit in waiting:
            quantise_group(unit)
        banks = (unit_bank, y_bank, unit_bank, turn_bank)
        before = []
        for n, unit in enumerate(unit_list(LAST_UNITS, counts)):
            multiply_unit(unit, banks[n % 4]())
            empty_unit(unit, LAST_ENGINES[n])
            for done in before:
                quantise_group(done)
            before = [unit]
        for done in before:
            quantise_group(done)
